import numpy as np, ml_dtypes
CORES = [83,85,87,115,117,119]
N = 6
BF = ml_dtypes.bfloat16
def gentries(a):
    return np.ascontiguousarray(a.reshape(8, 16, -1).transpose(0, 2, 1)).reshape(8, -1)
def gtable(e):
    e = np.asarray(e); return np.ascontiguousarray(e.reshape(8, -1, 16).transpose(0, 2, 1)).reshape(128, -1).astype(np.int32)
TT, P, R, S, CAP = 1024, 128, 3, 3, 16
def walk(planes, nbr, x, c):
    A = planes.astype(np.int64).reshape(N, 4, 4, TT).transpose(0, 3, 1, 2).reshape(N * TT, 4, 4); B = nbr.astype(np.int64).transpose(0, 2, 1).reshape(N * TT, 4)
    h = np.concatenate([x.astype(np.int64), np.ones((len(x), 1), np.int64)], 1); c = c.astype(np.int64); w = [c]
    for k in range(R):
        q = c // TT
        for s in range(S):
            v = np.einsum("mfc,mc->mf", A[c], h); face = np.argmin(v, 1)
            c = np.where((c // TT == q) & (np.min(v, 1) < 0), B[c, face], c)
        w.append(c)
    return np.stack(w)
def codes(rng, shape, own):
    r = np.arange(N).reshape(N, 1, 1); q = np.where(rng.random(shape) < own, r, (r + rng.integers(1, N, shape)) % N)
    return q * TT + rng.integers(0, TT, shape)
def mesh(rng, big, lo, hi):
    p = rng.integers(-big, big + 1, (N, 4, 4, TT)); p[:, :, 3] = rng.integers(lo, hi + 1, (N, 4, TT)); return p
def roomy(rng, p):
    h = np.stack([1 + rng.permutation(TT - 2)[:TT // 16] for r in range(N)]); k = h.shape[1]
    for r in range(N):
        u = p[r]; u[:, :3, h[r]] = rng.integers(-255, 256, (4, 3, k)); u[:, 3, h[r]] = rng.integers(3 * 255 * 1023, 2 ** 20 + 1, (4, k))
    return h
def choose(rng, p, h, b, x, c):
    big = int(np.abs(x).max()); r = np.arange(N).reshape(N, 1, 1)
    x = np.concatenate([x, rng.integers(-big, big + 1, (N, 8, P, 3))], 2); c = np.concatenate([c, r * TT + h[r, rng.integers(0, h.shape[1], (N, 8, P))]], 2)
    planes = p.reshape(N, 16, TT).astype(np.int32); m = c.shape[2]
    w = walk(planes, b, x.reshape(-1, 3), c.reshape(-1))[:R].reshape(R, N, 8, m) // TT
    cap = np.where(np.eye(N, dtype=bool), P, CAP); cnt = np.zeros((R, N, 8, N), np.int64); n = np.zeros((N, 8), np.int64); keep = np.zeros((N, 8, m), bool)
    k, i, g = np.ogrid[:R, :N, :8]
    for j in range(m):
        q = w[:, :, :, j]; ok = np.all(cnt[k, i, g, q] < cap[i, q], axis=0) & (n < P)
        cnt[k, i, g, q] += ok; n += ok; keep[:, :, j] = ok
    e = rng.permuted(np.nonzero(keep.reshape(N * 8, m))[1].reshape(N, 8, P), axis=2)
    x = np.take_along_axis(x, e[:, :, :, None], 2); c = np.take_along_axis(c, e, 2)
    return {"planes": planes, "nbr": b.astype(np.int32), "pts": np.ascontiguousarray(x.transpose(0, 1, 3, 2)).reshape(N, 24, P).astype(np.int32), "tet0": np.stack([gtable(u) for u in c])}
def setup_inputs(rng):
    p = mesh(rng, 127, -20000, 60000); h = roomy(rng, p)
    return choose(rng, p, h, codes(rng, (N, 4, TT), 0.6), rng.integers(-255, 256, (N, 8, 3 * P, 3)), codes(rng, (N, 8, 3 * P), 0.5))
def setup_inputs_full(rng):
    p = mesh(rng, 127, -20000, 60000); h = roomy(rng, p); r = np.arange(N).reshape(N, 1, 1); m = (N - 1) * CAP
    q = np.broadcast_to((r + 1 + np.arange(m) // CAP) % N, (N, 8, m)); c = q * TT + h[q, rng.integers(0, h.shape[1], (N, 8, m))]
    c = np.where(np.arange(8).reshape(1, 8, 1) % 2 == 0, c, codes(rng, (N, 8, m), 0.0)); c = np.concatenate([c, codes(rng, (N, 8, 2 * P), 0.8)], 2)
    return choose(rng, p, h, codes(rng, (N, 4, TT), 0.6), rng.integers(-255, 256, (N, 8, m + 2 * P, 3)), c)
def setup_inputs_ties(rng):
    p = mesh(rng, 1, -1, 2)
    p[:, 3] = np.where(rng.random((N, 1, TT)) < 0.5, p[:, 1], p[:, 3]); p[:, 2] = np.where(rng.random((N, 1, TT)) < 0.5, p[:, 0], p[:, 2]); h = roomy(rng, p)
    return choose(rng, p, h, codes(rng, (N, 4, TT), 0.6), rng.integers(-2, 3, (N, 8, 3 * P, 3)), codes(rng, (N, 8, 3 * P), 0.5))
def setup_inputs_few(rng):
    p = mesh(rng, 127, -20000, 60000); h = roomy(rng, p); b = codes(rng, (N, 4, TT), 1.0); q = rng.integers(0, N); b[q] = codes(rng, (N, 4, TT), 0.3)[q]
    c = codes(rng, (N, 8, 3 * P), 1.0); out = []
    for v in (b, c):
        u = rng.random(v.shape); out.append(np.where(u < 0.2, v // TT * TT, np.where(u < 0.4, v // TT * TT + TT - 1, v)))
    b, c = out; x = rng.integers(-255, 256, (N, 8, 3 * P, 3)); one = rng.random((N, 8, 3 * P)) < 0.4
    c = np.where(one, c[:, :, :1], c); x = np.where(one[:, :, :, None], x[:, :, :1], x)
    return choose(rng, p, h, b, x, c)
def setup_inputs_spread(rng):
    def some(bits, top, shape, plus):
        v = np.minimum(np.floor(np.exp2(bits * rng.random(shape))).astype(np.int64), top); v = np.where(rng.random(shape) < 0.125, top, v)
        return np.where(rng.random(shape) < plus, v, -v)
    p = some(10, 1023, (N, 4, 4, TT), 0.5); p[:, :, 3] = some(20, 2 ** 20, (N, 4, TT), 0.75); h = roomy(rng, p)
    return choose(rng, p, h, codes(rng, (N, 4, TT), 0.6), some(10, 1023, (N, 8, 3 * P, 3), 0.5), codes(rng, (N, 8, 3 * P), 0.5))
def points(pts, tet0):
    return pts.reshape(N, 8, 3, P).transpose(0, 1, 3, 2).reshape(-1, 3), np.stack([gentries(a) for a in tet0]).reshape(-1)
def check_inputs(d):
    bad = []; p = d["planes"].astype(np.int64).reshape(N, 4, 4, TT)
    if np.abs(p[:, :, :3]).max() > 1023 or np.abs(p[:, :, 3]).max() > 2 ** 20: bad.append("planes out of range")
    if np.abs(d["pts"].astype(np.int64)).max() > 1023: bad.append("pts out of range")
    for a in ("nbr", "tet0"):
        if d[a].min() < 0 or d[a].max() >= N * TT: bad.append(a + " out of range")
    if bad: return bad
    x, c = points(d["pts"], d["tet0"]); w = walk(d["planes"], d["nbr"], x, c)[:R].reshape(R, N, 8, P) // TT
    for q in range(N):
        n = np.count_nonzero(w == q, axis=3); n[:, q] = 0
        if n.max() > CAP: bad.append("more than CAP points of a group on rank " + str(q))
    return bad
def reference(planes, nbr, pts, tet0):
    x, c = points(pts, tet0); e = walk(planes, nbr, x, c)[R].reshape(N, 8, P)
    return {"y": np.stack([gtable(u) for u in e]).astype(np.float32)}

@@ -1,0 +1,534 @@
+from concourse.bass import DstId, RemoteDMATransfer
+from concourse.mybir import AluOpType, ActivationFunctionType
+
+N, TT, P, R, S = 6, 1024, 128, 3, 3
+OFF = 64
+TOP = TT + OFF
+W = TOP + 8
+FAR = 2048
+KEY = 16384.0
+BIG = 2.0 ** 37
+HOLD = 32768.0
+QB = 129
+BASE = QB - 1023.0 / 2048
+PRE = (2, 3)
+MIX = (((2, 1, 0, 0, 2, 0), (2, 1, 1, 0, 2, 0), (2, 1, 4, 7, 5)), ((0, 0, 1, 1, 1, 0), (2, 0, 0, 0, 2, 0), (2, 0, 1, 0, 1)))
+GAP0 = (9, 3)
+GAP = ((4, 6, 8, 3), (0, 0, 1, 1))
+
+
+def _s(n, dtype="float32"):
+    return ("sbuf", [128, n], dtype)
+
+
+SCRATCH = {
+    "PW": _s(W, "int32"), "NW": _s(W, "bfloat16"), "T0I": _s(8, "int32"),
+    "NT": _s(40, "int32"), "NA": _s(40, "int32"), "NU": _s(40), "NP": _s(80, "int32"), "NS": _s(120, "bfloat16"),
+    "ND": ("dram", [16, TT], "bfloat16"),
+    "P4": _s(32, "int32"), "P4H": _s(32, "float16"), "PD": _s(160, "float16"), "PT": _s(640), "PTH": _s(128),
+    "CI": _s(8, "int32"), "CF": _s(8), "C5": _s(3), "CX": _s(4), "IC": _s(128, "int32"), "ICM": _s(128, "int32"),
+    "MI": _s(128), "IA": _s(128), "IDS": _s(128), "IDH": _s(128, "float16"), "UT": _s(128, "bfloat16"),
+    "GS": _s(8), "GSL": _s(8), "GSH": _s(8, "float16"), "M48": _s(48), "G48": _s(48), "QC": _s(48), "CV": _s(48), "CJ": _s(48), "CJ0": _s(48),
+    "RKI": _s(40), "RNI": _s(40), "RK": _s(80), "RN0": _s(40, "bfloat16"), "RN1": _s(40, "bfloat16"), "RN2": _s(40, "bfloat16"),
+    "RNA": _s(40, "bfloat16"), "RNB": _s(40, "bfloat16"),
+    "CR": _s(80, "bfloat16"), "ON": _s(128, "bfloat16"), "R5": _s(80), "R6": _s(48),
+    "SA": _s(128, "int32"), "SB": _s(128, "int32"), "SV": _s(128), "SEL": _s(128, "float16"),
+    "NI": _s(4), "N6": _s(4, "int32"), "N6F": _s(4), "NM": _s(4), "NG": _s(4), "NK": _s(4),
+    "L6": _s(4, "uint16"), "LR": _s(4, "uint16"), "LA": _s(8, "uint16"), "LD": _s(8, "uint16"), "LT": _s(8, "uint16"),
+    "HL": _s(8, "uint16"), "GL": _s(8, "uint16"), "JL": _s(8, "uint16"),
+    "US": _s(48), "QI": _s(48, "bfloat16"), "OH": _s(48, "bfloat16"), "VV": _s(48), "BT": _s(96, "float16"), "SS": _s(48),
+    "AA": _s(128, "float16"), "AT": _s(128), "M12": _s(12), "MK": _s(24), "TM": _s(24), "CHB": _s(48), "RX": _s(48), "DX": _s(128), "YS": _s(8),
+    "GT": _s(80), "GDF": _s(128),
+}
+for _t in "HG":
+    _n = 128 if _t == "H" else 80
+    SCRATCH.update({_t + "P": _s(_n), _t + "N": _s(_n, "bfloat16"), _t + "SC": _s(80), _t + "D0": _s(40), _t + "D1": _s(40),
+                    _t + "Z": _s(40), _t + "D": _s(128, "float16"), _t + "V0": _s(40 if _t == "G" else 8), _t + "V1": _s(40 if _t == "G" else 8)})
+for _k in range(R):
+    SCRATCH["MS%d" % _k] = _s(12, "float16")
+    SCRATCH["LM%d" % _k] = _s(10, "float16")
+    SCRATCH["RT%d" % _k] = _s(8)
+    SCRATCH["RL%d" % _k] = _s(8)
+for _k in range(8):
+    SCRATCH["b%d" % _k] = ("psum", [128, 512], "float32")
+
+SEMAPHORES = ["v", "t", "s", "c", "ltet", "lpts", "lpl", "lnt", "lnd", "lnb", "sty", "pd", "sent"] + ["rq%d" % k for k in range(R)] + ["rt%d" % k for k in range(R)]
+BANKS = ["b%d" % k for k in range(8)]
+
+
+def slot(owner, other):
+    return other - (1 if other > owner else 0)
+
+
+def engine_split(topo, src, dsts):
+    on = [d for d in dsts if topo.chip(d) == topo.chip(src)]
+    off = [d for d in dsts if topo.chip(d) != topo.chip(src)]
+    eo = topo.engines(src, off[0])
+    out = {}
+    for ds, es in ((off, eo), (on, [e for e in topo.engines(src, on[0]) if e not in eo])):
+        per = 1
+        while 2 * per * len(ds) <= len(es):
+            per *= 2
+        for i, d in enumerate(ds):
+            out[d] = es[i * per:(i + 1) * per]
+    return out
+
+
+def rank_program(g, core, T, topo):
+    me = T.rank_of(core)
+    if me is None:
+        return
+    cores = list(T.cores)
+    others = [q for q in range(N) if q != me]
+    op = AluOpType
+    act = ActivationFunctionType
+    rel = float(OFF - TT * me)
+
+    queues = {"v": g.vector, "t": g.tensor, "s": g.scalar, "c": g, "y": g.sync}
+    known = {q: {} for q in queues}
+    count = {q: 0 for q in queues}
+    clocks, writers, readers = {}, {}, {}
+
+    def wait(q, s, n):
+        queues[q].wait_ge(T.sem[s], n)
+        for a, b in clocks[(s, n)].items():
+            known[q][a] = max(b, known[q].get(a, 0))
+
+    def need(q, r, w):
+        ev = []
+        for k in r:
+            ev += writers.get(k, [])
+            if k in BANKS:
+                ev += [e for e in readers.get(k, []) if e[0] != q]
+        for k in w:
+            ev += writers.get(k, [])
+            ev += [e for e in readers.get(k, []) if e[0] != q]
+        top = {}
+        for s, n in ev:
+            if not (q == "t" and s == "t"):
+                top[s] = max(n, top.get(s, 0))
+        for s, n in sorted(top.items(), key=lambda e: e[0]):
+            if known[q].get(s, 0) >= n:
+                continue
+            if any(o != s and known[q].get(o, 0) < m and clocks[(o, m)].get(s, 0) >= n for o, m in top.items()):
+                continue
+            wait(q, s, n)
+
+    def do(q, fn, r, w):
+        r, w = r.split(), w.split()
+        need(q, r, w)
+        fn(queues[q]).then_inc(T.sem[q], 1)
+        count[q] += 1
+        ev = (q, count[q])
+        clocks[ev] = dict(known[q])
+        clocks[ev][q] = count[q]
+        for k in r:
+            readers.setdefault(k, []).append(ev)
+        for k in w:
+            writers[k] = [ev]
+            readers[k] = []
+
+    def event(sem, total, w):
+        clocks[(sem, total)] = {sem: total}
+        for k in w.split():
+            writers[k] = [(sem, total)]
+            readers[k] = []
+
+    def dma(q, sem, out, in_, r="", w=""):
+        need(q, r.split(), w.split())
+        queues[q].dma_start(out, in_).then_inc(T.sem[sem], 16)
+
+    def tt(out, a, b, o, r, w):
+        do("v", lambda e: e.tensor_tensor(out=out, in0=a, in1=b, op=o), r, w)
+
+    def ts(out, a, s1, o0, r, w, s2=None, o1=None):
+        if o1 is None:
+            do("v", lambda e: e.tensor_scalar(out, a, s1, None, op0=o0), r, w)
+        else:
+            do("v", lambda e: e.tensor_scalar(out, a, s1, s2, op0=o0, op1=o1), r, w)
+
+    def cp(out, a, r, w):
+        do("v", lambda e: e.tensor_copy(out, a), r, w)
+
+    def fill(ap, x, w):
+        do("v", lambda e: e.memset(ap, x), "", w)
+
+    def sc(out, a, r, w, bias=0.0, scale=1.0, f=act.Copy):
+        do("s", lambda e: e.activation(out, a, f, bias=bias, scale=scale), r, w)
+
+    def sfill(ap, n, x, w):
+        sc(ap, T.R6[:, 0:n], "R6", w, bias=x, scale=0.0)
+
+    def scan(out, d0, d1, o0, o1, r, w):
+        do("v", lambda e: e.tensor_tensor_scan(out, d0, d1, 0.0, o0, o1), r, w)
+
+    def mm(out, lhsT, rhs, start, stop, r, w):
+        do("t", lambda e: e.matmul(out, lhsT, rhs, start, stop), r, w)
+
+    def iota(out, pattern, base, cm, w, small=True):
+        if small:
+            do("c", lambda e: e.iota(out, pattern, base, cm, allow_small_or_imprecise_dtypes=True), "", w)
+        else:
+            do("c", lambda e: e.iota(out, pattern, base, cm), "", w)
+
+    split = engine_split(topo, core, [cores[q] for q in others])
+    into = sum(len(engine_split(topo, cores[q], [c for c in cores if c != cores[q]])[core]) for q in others)
+    sent = [0]
+
+    def send(src, dst, sem, r):
+        need("c", r.split(), [])
+        tr = []
+        for q in others:
+            rid, pid = topo.addr(cores[q])[:2]
+            tr.append(RemoteDMATransfer(dst_ids=[DstId(rid=rid, pnc=pid)], dma_engine_mask=sum(1 << e for e in split[cores[q]]),
+                                        remote_sem=T.sem[sem], src=src(q), dst=dst(q)))
+            sent[0] += len(split[cores[q]])
+        g.remote_dma_fused(tr, local_sem=T.sem.sent)
+
+    fill(T.P4[:, :], 0, "P4")
+    dma("y", "ltet", T.T0I[:, :], T.tet0[:, :])
+    dma("s", "lnt", T.NT[:, 0:32], T.nbr[:, :])
+    for b in range(4):
+        dma("y" if b % 2 else "s", "lpts", T.P4[32 * b:32 * b + 24, :], T.pts[:, 32 * b:32 * b + 32], "", "P4")
+    for k in range(8):
+        dma("y" if k % 2 else "s", "lpl", T.PW[16 * k:16 * k + 16, OFF:TOP], T.planes[:, :])
+
+    fill(T.R6[:, :], 1.0, "R6")
+    fill(T.ON[:, :], 1.0, "ON")
+    iota(T.CI[:, 0:1], [[0, 1]], 0, 1, "CI0", small=False)
+    iota(T.IC[:, :], [[1, 128]], 0, 0, "IC", small=False)
+    iota(T.NT[:, 32:40], [[1, 8]], TT * me, 8, "NT1", small=False)
+    iota(T.QC[:, :], [[0, 8], [1, 6]], QB, 0, "QC")
+    do("c", lambda e: e.affine_select(T.UT[:, :], T.ON[:, :], [[1, 128]], op.is_gt, 0.0, 0, -1), "ON", "UT")
+    do("c", lambda e: e.affine_select(T.UT[:, :], T.UT[:, :], [[1, 128]], op.not_equal, 256.0, 0, -1), "UT", "UT")
+    iota(T.RKI[:, :], [[4, 8], [-1, 5]], 4, 0, "RKI")
+    event("ltet", 16, "T0I")
+    event("lnt", 16, "NT0")
+    event("lpts", 64, "P4")
+    event("lpl", 128, "PWa")
+
+    fill(T.R6[:, 0::6], 0.0, "R6")
+    for ap, n, x, w in ((T.GZ[:, :], 40, 0.0, "GZ"), (T.GV0[:, :], 40, 0.0, "GV0"), (T.GV1[:, :], 40, 0.0, "GV1"), (T.R5[:, 0::2], 40, 2 * BIG, "R5"),
+                        (T.R5[:, 1::2], 40, KEY / 2, "R5"), (T.R5[:, 0::10], 8, -BIG, "R5"), (T.R5[:, 1::10], 8, -BIG - KEY, "R5"),
+                        (T.CR[:, 0::2], 40, KEY / 2, "CR"), (T.CR[:, 1::2], 40, -KEY / 2, "CR"), (T.CR[:, 0::10], 8, 2 * BIG, "CR"),
+                        (T.CR[:, 1::10], 8, BIG, "CR")):
+        sfill(ap, n, x, w)
+    rs, an = op.arith_shift_right, op.bitwise_and
+    ts(T.CI[:, 1:2], T.CI[:, 0:1], 15, an, "CI0", "CI1")
+    ts(T.CI[:, 2:3], T.CI[:, 0:1], 4, rs, "CI0", "CI2")
+    ts(T.CI[:, 3:4], T.CI[:, 0:1], 2, rs, "CI0", "CI3")
+    ts(T.CI[:, 4:5], T.CI[:, 0:1], 4, rs, "CI0", "CI4", 1, an)
+    ts(T.CI[:, 5:6], T.CI[:, 0:1], 3, an, "CI0", "CI5")
+    ts(T.CI[:, 6:7], T.CI[:, 0:1], 5, rs, "CI0", "CI6")
+    ts(T.CI[:, 7:8], T.CI[:, 0:1], 31, an, "CI0", "CI7")
+    ts(T.ICM[:, :], T.IC[:, :], 15, an, "IC", "ICM")
+    cp(T.CF[:, :], T.CI[:, :], "CI0 CI1 CI2 CI3 CI4 CI5 CI6 CI7", "CF")
+    p, p15, pg, p2, podd, p3, p5, p31 = [T.CF[:, k:k + 1] for k in range(8)]
+    cp(T.LT[:, :], T.IC[:, 0:8], "IC", "LT")
+    ts(T.MI[:, :], T.ICM[:, :], p15, op.is_equal, "ICM CF", "MI")
+    ts(T.GS[:, :], T.IC[:, 0:8], pg, op.is_equal, "IC CF", "GS")
+    ts(T.NI[:, 0:3], T.IC[:, 0:3], 16.0, op.mult, "IC CF", "NI", p15, op.add)
+    ts(T.N6[:, 0:3], T.NI[:, 0:3], 1.0 / 6, op.mult, "NI", "N6", -2.5 / 6, op.add)
+    ts(T.L6[:, 0:3], T.N6[:, 0:3], 6.0, op.mult, "N6", "L6", 5.0, op.add)
+
+    cp(T.P4H[:, :], T.P4[:, :], "P4", "P4H")
+    send(lambda q: T.P4H[:, :], lambda q: T.PD[:, 32 * slot(q, me):32 * slot(q, me) + 32], "pd", "P4H")
+    event("pd", into, "PD")
+    iota(T.RNI[:, :], [[16, 8], [-1, 5]], 4, 0, "RNI")
+    iota(T.C5[:, :], [[-5, 3]], 0, 1, "C5")
+    iota(T.G48[:, :], [[1, 8], [0, 6]], 0, 0, "G48")
+
+    def spread(bank, at, n, src, b):
+        mm(T[bank][:, at:at + n], T.SEL[32 * b:32 * b + 32, :], T[src][32 * b:32 * b + 32, :], True, True, src + " SEL", bank)
+
+    def guest_points():
+        for b, bank in enumerate(("b0", "b1", "b2", "b6")):
+            spread(bank, 0, 160, "PD", b)
+        for b, bank in ((0, "b0"), (2, "b2")):
+            sc(T.PT[:, 160 * b:160 * b + 160], T[bank][:, 0:160], bank + " CX2", "PT%d" % b, bias=T.CX[:, 2:3], f=act.Identity)
+        yield
+        for b, bank in ((1, "b1"), (3, "b6")):
+            ts(T.PT[:, 160 * b:160 * b + 160], T[bank][:, 0:160], T.CX[:, 2:3], op.add, bank + " CX2", "PT%d" % b)
+        yield
+
+    def window():
+        for b in (1, 2, 0):
+            r = "NS%d" % b
+            dma("y", "lnd", T.ND[5 * b:5 * b + 4, :], T.NS[:, 40 * b:40 * b + 32], r)
+            dma("s", "lnd", T.ND[5 * b + 4:5 * b + 5, :], T.NS[:, 40 * b + 32:40 * b + 40], r)
+        dma("y", "lnd", T.ND[15:16, :], T.NS[:, 112:120], "NS2")
+        event("lnd", 7 * 16, "ND")
+        for k in range(8):
+            dma("y", "lnb", T.NW[16 * k:16 * k + 16, OFF:TOP], T.ND[:, :], "ND")
+        event("lnb", 128, "NWa")
+
+    def constants():
+        fill(T.US[:, :], 0.0, "US")
+        yield
+        ts(T.NA[:, :], T.NT[:, :], 10, rs, "NT0 NT1", "NA")
+        yield
+        fill(T.QI[:, :], 0.0, "QI")
+        yield
+        ts(T.NP[:, 40:80], T.NT[:, :], 63, an, "NT0 NT1", "NP1")
+        yield
+        ts(T.NU[:, :], T.NA[:, :], float(me), op.is_equal, "NA", "NU", FAR - rel, op.mult)
+        yield
+        ts(T.NP[:, 0:40], T.NT[:, :], 8192 - 64, an, "NT0 NT1", "NP0")
+        yield
+        cp(T.NS[:, 40:80], T.NP[:, 40:80], "NP1", "NS1")
+        yield
+        ts(T.NS[:, 80:120], T.NU[:, :], float(-FAR), op.add, "NU", "NS2")
+        yield
+        ts(T.CV[:, :], T.QC[:, :], -1.0, op.mult, "QC", "CV", QB - BASE + OFF / float(TT), op.add)
+        yield
+        ts(T.CJ0[:, :], T.QC[:, :], float(QB + me), op.is_lt, "QC", "CJ0", -32.0, op.mult)
+        yield
+        tt(T.NS[:, 0:40], T.NP[:, 0:40], T.NS[:, 80:120], op.subtract, "NP0 NS2", "NS0")
+        window()
+        yield
+        ts(T.CX[:, 0:1], p5, 160.0, op.mult, "CF", "CX0", p31, op.add)
+        yield
+        ts(T.CJ[:, :], T.CJ0[:, :], T.CX[:, 0:1], op.add, "CJ0 CX0", "CJ", 32.0 * me, op.add)
+        yield
+        ts(T.LA[:, :], T.IC[:, 0:8], 6.0, op.mult, "IC", "LA", 5.0, op.add)
+        yield
+        ts(T.IA[:, :], T.ICM[:, :], 256.0, op.add, "ICM", "IA")
+        yield
+        ts(T.SA[:, :], T.IC[:, :], 4, rs, "IC", "SA")
+        yield
+        ts(T.SB[:, :], T.IC[:, :], 3, an, "IC", "SB")
+        yield
+        ts(T.SV[:, :], T.SA[:, :], 3.0, op.mult, "SA", "SV")
+        yield
+        ts(T.CX[:, 1:2], podd, -1.0, op.mult, "CF", "CX1", 1.0, op.add)
+        yield
+        tt(T.SV[:, :], T.SV[:, :], T.SB[:, :], op.add, "SV SB", "SV")
+        yield
+        fill(T.M12[:, 0::2], float(TT), "M12a")
+        yield
+        fill(T.M12[:, 1::2], 1.0, "M12b")
+        yield
+        fill(T.SV[:, 3::4], -1000.0, "SV")
+        yield
+        ts(T.MK[:, 0:12], T.M12[:, :], T.CX[:, 1:2], op.mult, "M12a M12b CX1", "MK0")
+        yield
+        ts(T.MK[:, 12:24], T.M12[:, :], podd, op.mult, "M12a M12b CF", "MK1")
+        yield
+        ts(T.SEL[:, :], T.SV[:, :], p31, op.is_equal, "SV CF", "SEL")
+        yield
+        ts(T.CX[:, 2:3], p3, 3.0, op.is_equal, "CF", "CX2")
+        for b in range(4):
+            if b:
+                wait("t", "t", count["t"])
+            spread("b3", 32 * b, 32, "P4H", b)
+        sc(T.PTH[:, :], T.b3[:, 0:128], "b3 CX2", "PTH", bias=T.CX[:, 2:3], f=act.Identity)
+        yield
+        ts(T.RK[:, 0::2], T.RKI[:, :], p2, op.is_equal, "RKI CF", "RKa", -KEY, op.mult)
+        yield
+        ts(T.RK[:, 1::2], T.RKI[:, :], p2, op.is_equal, "RKI CF", "RKb", KEY, op.mult)
+        yield
+        fill(T.RK[:, 0::10], 0.0, "RKa")
+        yield
+        fill(T.RK[:, 1::10], 0.0, "RKb")
+        yield
+        ts(T.HL[:, :], T.T0I[:, :], rel, op.add, "T0I", "HL", float(TOP), op.min)
+        yield
+        fill(T.PW[:, 0:OFF], 0, "PWb0")
+        yield
+        fill(T.PW[:, TOP:W], 0, "PWb1")
+        yield
+        fill(T.NW[:, 0:OFF], 0.0, "NWp0")
+        yield
+        fill(T.NW[:, TOP:W], 0.0, "NWp1")
+        yield
+        ts(T.IDS[:, :], T.IC[:, :], p, op.is_equal, "IC CF", "IDS", 1.0 / TT, op.mult)
+        yield
+        ts(T.RN0[:, :], T.RNI[:, :], T.C5[:, 0:1], op.is_equal, "RNI C5", "RN0")
+        yield
+        ts(T.RN1[:, :], T.RNI[:, :], T.C5[:, 1:2], op.is_equal, "RNI C5", "RN1")
+        yield
+        tt(T.RNA[:, :], T.RN0[:, :], T.RN1[:, :], op.add, "RN0 RN1", "RNA")
+        yield
+        ts(T.GSH[:, :], T.IC[:, 0:8], pg, op.is_equal, "IC CF", "GSH")
+        yield
+        ts(T.LD[:, :], T.IC[:, 0:8], 5.0, op.mult, "IC", "LD", 4.0, op.add)
+        yield
+
+    def dispatch(k, more):
+        ms = "MS%d" % k
+
+        def gap(i):
+            for _ in range(GAP[min(k, 1)][i]):
+                next(more, None)
+
+        tt(T.OH[:, :], T.QI[:, :].indirect(T.L6[:, 0:3]), T.QC[:, :], op.is_equal, "QI L6 QC", "OH")
+        mm(T.b7[:, 0:48], T.UT[:, :], T.OH[:, :], True, True, "UT OH", "b7")
+        if k:
+            scan(T.US[:, :], T.R6[:, :], T.b6[:, 128:176], op.mult, op.max, "R6 b6", "US")
+        gap(0)
+        tt(T.BT[:, 1::2], T.CJ[:, :], T.OH[:, :], op.mult, "CJ OH", "BTj")
+        tt(T.VV[:, :], T.US[:, :].indirect(T.L6[:, 0:3]), T.CV[:, :], op.add, "US L6 CV", "VV")
+        scan(T.SS[:, :], T.R6[:, :], T.b7[:, 0:48], op.mult, op.max, "R6 b7", "SS")
+        gap(1)
+        tt(T.BT[:, 0::2], T.VV[:, :], T.OH[:, :], op.mult, "VV OH", "BTt")
+        tt(T.AA[:, :], T.SS[:, :].indirect(T.LA[:, 0:8]), T.IA[:, :], op.is_equal, "SS LA IA", "AA")
+        for a in range(4):
+            mm(T.b7[32 * a:32 * a + 32, 64:88], T.AA[:, 32 * a:32 * a + 32], T.BT[:, 24 * a:24 * a + 24], True, True, "AA BTj BTt", "b7")
+        gap(2)
+        tt(T.TM[:, :], T.b7[:, 64:88], T.MK[:, :], op.mult, "b7 MK0 MK1", "TM")
+        gap(3)
+        tt(T[ms][:, :], T.TM[:, 0:12], T.TM[:, 12:24], op.add, "TM", ms)
+        send(lambda q: T[ms][:, 2 * q:2 * q + 2], lambda q: T["LM%d" % k][:, 2 * slot(q, me):2 * slot(q, me) + 2], "rq%d" % k, ms)
+        event("rq%d" % k, into, "LM%d" % k)
+
+    def hold():
+        ts(T.CHB[:, :], T.OH[:, :], HOLD, op.mult, "OH", "CHB", TT * BASE - HOLD, op.add)
+
+    def turn():
+        mm(T.b6[:, 0:128], T.AA[:, :], T.IDH[:, :], True, True, "AA IDH", "b6")
+        sc(T.AT[:, :], T.b6[:, 0:128], "b6", "AT")
+
+    def step(h, i):
+        last = i == S - 1
+        n, lst, pt, bk, bn, bc = (128, T.HL[:, 0:8], "PTH", "b3", "b4", "b5") if h == "H" else (80, T.GL[:, 0:5], "GT", "b0", "b1", "b2")
+        ln, m = h + "L", n // 16
+        X = lambda a: T[h + a]
+        ones = lambda: mm(T[bk][0:n, 0:80], T.ON[0:1, 0:n], T.CR[0:1, :], True, False, "ON CR", bk)
+        left = lambda j: mm(T[bn][0:n, 0:40], T.IDS[0:n, 0:n], X("V%d" % j)[0:n, :], not j, False, "IDS " + h + "V%d" % j, bn)
+        if not i:
+            ones()
+        sc(X("N")[:, :], T.NW[:, :].indirect(lst), "NWp0 NWp1 NWa " + ln, h + "N")
+        tt(X("P")[:, :], T.PW[:, :].indirect(lst), T[pt][:, 0:n], op.mult, "PWa PWb0 PWb1 " + ln + " " + pt, h + "P")
+        mm(T[bk][0:n, 0:80], X("P")[:, :], T.RK[:, :], False, True, h + "P RKa RKb", bk)
+        if last:
+            mm(T[bn][0:n, 0:40], X("N")[:, :], T.RNB[:, :], h == "H", True, h + "N RNB", bn)
+        else:
+            mm(T[bn][0:n, 0:40], X("N")[:, :], T.RNA[:, :], True, True, h + "N RNA", bn)
+        yield
+        scan(X("SC")[0:n, :], T.R5[0:n, :], T[bk][0:n, 0:80], op.min, op.add, "R5 " + bk, h + "SC")
+        if h == "G":
+            sc(X("D0")[0:n, :], X("SC")[0:n, 0::2], h + "SC", h + "D0", scale=-1.0)
+        if not last:
+            ones()
+        yield
+        tt(X("D1")[0:n, :], X("SC")[0:n, 0::2], T[bn][0:n, 0:40], op.min, h + "SC " + bn, h + "D1")
+        if h == "H":
+            ts(X("D0")[0:n, :], X("SC")[0:n, 0::2], -1.0, op.mult, h + "SC", h + "D0")
+        if h == "G" and i == S - 2:
+            left(0)
+        yield
+        if h == "H" and i:
+            tt(T.CHB[:, me::6], T.CHB[:, me::6], T["HV%d" % (i - 1)][:, :], op.add, "CHB HV%d" % (i - 1), "CHB")
+        scan(X("Z")[0:n, :], X("D0")[0:n, :], X("D1")[0:n, :], op.min, op.max, h + "D0 " + h + "D1", h + "Z")
+        yield
+        if not last:
+            v, c = (T["HV%d" % i][:, :], 1) if h == "H" else (T["GV%d" % i][0:n, 0::5], TT)
+            sc(v, X("Z")[0:n, 4::5], h + "Z", h + "V%d" % i, bias=float(-FAR * c), scale=float(c), f=act.Relu)
+            tt(X("D")[:, :], X("Z")[:, :].indirect(T.LD[:, 0:8]), T.MI[:, :], op.mult, h + "Z LD MI", h + "D")
+            mm(T[bc][:, 0:m], X("D")[0:n, :], T.GSH[0:n, 0:m], True, True, h + "D GSH", bc)
+            if h == "G" and i == S - 2:
+                left(1)
+            yield
+            ts(lst, T[bc][:, 0:m], float(TOP), op.min, bc, ln)
+            yield
+        elif h == "H":
+            tt(T.CHB[:, me::6], T.CHB[:, me::6], T.HZ[:, 4::5], op.add, "CHB HZ", "CHB")
+            yield
+        else:
+            tt(T.GDF[:, :], T.GZ[:, :].indirect(T.LD[:, 0:8]), T.MI[:, :], op.mult, "GZ LD MI", "GDF")
+            mm(T[bc][:, 0:m], T.GDF[0:n, :], T.GS[0:n, 0:m], True, True, "GDF GS", bc)
+            yield
+
+    def home(k):
+        if k:
+            to_list()
+            yield
+            hold()
+            turn()
+            yield
+            ts(T.HL[:, :], T.b5[:, 0:8], rel - TT * BASE, op.add, "b5", "HL", float(TOP), op.min)
+            yield
+        for i in range(S):
+            for _ in step("H", i):
+                yield
+
+    def guests(k, own):
+        lm = "LM%d" % k
+        cp(T.JL[:, 0:5], T[lm][:, 1::2], lm, "JL")
+        sc(T.GT[:, :], T.PT[:, :].indirect(T.JL[:, 0:5]), "PT0 PT1 PT2 PT3 JL", "GT")
+        cp(T.GL[:, 0:5], T[lm][:, 0::2], lm, "GL")
+        for i in range(S):
+            mine = step("G", i)
+            for pieces in MIX[min(k, 1)][i]:
+                next(mine, None)
+                for _ in range(pieces):
+                    next(own, None)
+            for _ in mine:
+                pass
+        cp(T["RT%d" % k][:, 0:5], T.b2[:, 0:5], "b2", "RT%d" % k)
+        send(lambda q: T["RT%d" % k][:, slot(me, q):slot(me, q) + 1], lambda q: T["RL%d" % k][:, slot(q, me):slot(q, me) + 1], "rt%d" % k, "RT%d" % k)
+        event("rt%d" % k, into, "RL%d" % k)
+
+    def replies(k):
+        mm(T.b6[:, 128:176], T.IDS[:, :], T.CHB[:, :], True, False, "IDS CHB", "b6")
+        tt(T.RX[:, :], T["RL%d" % k][:, 0:5].indirect(T.LR[:, 0:3]), T.M48[:, :], op.mult, "RL%d LR M48" % k, "RX")
+        mm(T.b6[:, 128:176], T.AT[:, :], T.RX[:, :], False, True, "AT RX", "b6")
+        if k < R - 1:
+            scan(T.QI[:, :], T.R6[:, :], T.b6[:, 128:176], op.mult, op.max, "R6 b6", "QI")
+        else:
+            scan(T.US[:, :], T.R6[:, :], T.b6[:, 128:176], op.mult, op.max, "R6 b6", "US")
+
+    def to_list():
+        tt(T.DX[:, :], T.US[:, :].indirect(T.LA[:, 0:8]), T.MI[:, :], op.mult, "US LA MI", "DX")
+        mm(T.b5[:, 0:8], T.DX[:, :], T.GSL[:, :], True, True, "DX GSL", "b5")
+
+    tt(T.DX[:, :], T.T0I[:, :].indirect(T.LT[:, 0:8]), T.MI[:, :], op.mult, "T0I LT MI", "DX")
+    mm(T.b7[:, 0:8], T.DX[:, :], T.GS[:, :], True, True, "DX GS", "b7")
+    first = constants()
+    for _ in range(GAP0[0]):
+        next(first)
+    ts(T.QI[:, 5::6], T.b7[:, 0:8], 1.0 / TT, op.mult, "b7", "QI", BASE, op.add)
+    for _ in range(GAP0[1]):
+        next(first)
+    ts(T.US[:, 5::6], T.b7[:, 0:8], 1.0 / TT, op.mult, "b7", "US", BASE, op.add)
+    dispatch(0, first)
+    for _ in first:
+        pass
+    ts(T.RN2[:, :], T.RNI[:, :], T.C5[:, 2:3], op.is_equal, "RNI C5", "RN2")
+    tt(T.RNB[:, :], T.RNA[:, :], T.RN2[:, :], op.add, "RNA RN2", "RNB")
+    ts(T.IDH[:, :], T.IC[:, :], p, op.is_equal, "IC CF", "IDH")
+    hold()
+    turn()
+
+    own, points = home(0), guest_points()
+    next(points)
+    for k in range(R):
+        for i in range(PRE[min(k, 1)]):
+            next(own, None)
+            next(points, None)
+        guests(k, own)
+        if k == 0:
+            ts(T.M48[:, :], T.G48[:, :], pg, op.is_equal, "G48 CF", "M48", 1.0 / TT, op.mult)
+            fill(T.M48[:, me::6], 0.0, "M48")
+            ts(T.N6F[:, 0:3], T.N6[:, 0:3], -6.0, op.mult, "N6", "N6F")
+            tt(T.NM[:, 0:3], T.NI[:, 0:3], T.N6F[:, 0:3], op.add, "NI N6F", "NM")
+            ts(T.NG[:, 0:3], T.NM[:, 0:3], float(me), op.is_gt, "NM", "NG")
+            tt(T.NK[:, 0:3], T.NM[:, 0:3], T.NG[:, 0:3], op.subtract, "NM NG", "NK")
+            ts(T.LR[:, 0:3], T.NK[:, 0:3], 4.0, op.min, "NK", "LR")
+            ts(T.GSL[:, :], T.GS[:, :], float(TT), op.mult, "GS", "GSL")
+        for _ in own:
+            pass
+        replies(k)
+        if k < R - 1:
+            own = home(k + 1)
+            dispatch(k + 1, own)
+
+    to_list()
+    ts(T.YS[:, :], T.b5[:, 0:8], -TT * BASE, op.add, "b5", "YS")
+    dma("y", "sty", T.y[:, :], T.YS[:, :], "YS")
+
+    g.wait_ge(T.sem.sty, 16)
+    g.wait_ge(T.sem.sent, sent[0])
+    for q in "vtsc":
+        if known["c"].get(q, 0) < count[q]:
+            g.wait_ge(T.sem[q], count[q])

@@ -8,13 +8,10 @@ W = TOP + 8
 FAR = 2048
 KEY = 16384.0
 BIG = 2.0 ** 37
-HOLD = 32768.0
-QB = 129
-BASE = QB - 1023.0 / 2048
-PRE = (2, 3)
-MIX = (((2, 1, 0, 0, 2, 0), (2, 1, 1, 0, 2, 0), (2, 1, 4, 7, 5)), ((0, 0, 1, 1, 1, 0), (2, 0, 0, 0, 2, 0), (2, 0, 1, 0, 1)))
-GAP0 = (9, 3)
-GAP = ((4, 6, 8, 3), (0, 0, 1, 1))
+MID = 511.5
+QB = 129.0
+CYC = 1.04e-3
+LAT, LOCAL, HOP, ISSUE, FIRST = 0.11, 1.6, 1.9, 0.5, 1.0
 
 
 def _s(n, dtype="float32"):
@@ -23,41 +20,43 @@ def _s(n, dtype="float32"):
 
 SCRATCH = {
     "PW": _s(W, "int32"), "NW": _s(W, "bfloat16"), "T0I": _s(8, "int32"),
-    "NT": _s(40, "int32"), "NA": _s(40, "int32"), "NU": _s(40), "NP": _s(80, "int32"), "NS": _s(120, "bfloat16"),
-    "ND": ("dram", [16, TT], "bfloat16"),
-    "P4": _s(32, "int32"), "P4H": _s(32, "float16"), "PD": _s(160, "float16"), "PT": _s(640), "PTH": _s(128),
-    "CI": _s(8, "int32"), "CF": _s(8), "C5": _s(3), "CX": _s(4), "IC": _s(128, "int32"), "ICM": _s(128, "int32"),
-    "MI": _s(128), "IA": _s(128), "IDS": _s(128), "IDH": _s(128, "float16"), "UT": _s(128, "bfloat16"),
-    "GS": _s(8), "GSL": _s(8), "GSH": _s(8, "float16"), "M48": _s(48), "G48": _s(48), "QC": _s(48), "CV": _s(48), "CJ": _s(48), "CJ0": _s(48),
-    "RKI": _s(40), "RNI": _s(40), "RK": _s(80), "RN0": _s(40, "bfloat16"), "RN1": _s(40, "bfloat16"), "RN2": _s(40, "bfloat16"),
-    "RNA": _s(40, "bfloat16"), "RNB": _s(40, "bfloat16"),
+    "NT": _s(64, "int32"), "NA": _s(64, "int32"), "NU": _s(64), "NP": _s(128, "int32"), "NS": _s(192, "bfloat16"),
+    "ND": _s(TT, "bfloat16"), "MIH": _s(128, "bfloat16"),
+    "P4": _s(32, "int32"), "PD": _s(192, "float16"), "PTA": _s(768), "PTB": _s(1024), "QR": _s(1024, "float16"),
+    "PQ": _s(128, "int32"), "PQH": _s(128, "float16"), "HTA": _s(128), "HTB": _s(128), "IW": _s(768),
+    "PO": _s(4), "PR": _s(4), "CX": _s(8), "DC": _s(128), "M2": _s(128), "E48": _s(48), "KD": _s(128), "FK": _s(40), "FB": _s(40), "C26": _s(8),
+    "CI": _s(10, "int32"), "CF": _s(10), "IC": _s(128, "int32"), "IC3": _s(128, "int32"), "SEL": _s(512, "float16"),
+    "MI": _s(128), "MIP": _s(128), "MI8": _s(128), "IA": _s(128), "IDF": _s(128), "IDH": _s(128, "float16"), "IDP": _s(128), "IDQ": _s(128, "float16"),
+    "UT": _s(128, "bfloat16"), "GSH": _s(8, "bfloat16"), "GSP": _s(8, "bfloat16"), "GS48": _s(48), "CY": _s(48), "ONF": _s(128),
+    "RK1": _s(40), "RK": _s(80), "RN0": _s(40), "RN1": _s(40), "RN2": _s(40), "RNA": _s(40, "bfloat16"), "RNB": _s(40, "bfloat16"),
     "CR": _s(80, "bfloat16"), "ON": _s(128, "bfloat16"), "R5": _s(80), "R6": _s(48),
-    "SA": _s(128, "int32"), "SB": _s(128, "int32"), "SV": _s(128), "SEL": _s(128, "float16"),
-    "NI": _s(4), "N6": _s(4, "int32"), "N6F": _s(4), "NM": _s(4), "NG": _s(4), "NK": _s(4),
-    "L6": _s(4, "uint16"), "LR": _s(4, "uint16"), "LA": _s(8, "uint16"), "LD": _s(8, "uint16"), "LT": _s(8, "uint16"),
-    "HL": _s(8, "uint16"), "GL": _s(8, "uint16"), "JL": _s(8, "uint16"),
-    "US": _s(48), "QI": _s(48, "bfloat16"), "OH": _s(48, "bfloat16"), "VV": _s(48), "BT": _s(96, "float16"), "SS": _s(48),
-    "AA": _s(128, "float16"), "AT": _s(128), "M12": _s(12), "MK": _s(24), "TM": _s(24), "CHB": _s(48), "RX": _s(48), "DX": _s(128), "YS": _s(8),
-    "GT": _s(80), "GDF": _s(128),
+    "LA": _s(8, "uint16"), "LD": _s(8, "uint16"), "LT": _s(8, "uint16"), "LP": _s(8, "uint16"), "LI": _s(8, "uint16"),
+    "HL": _s(8, "uint16"), "GLA": _s(8, "uint16"), "JLA": _s(8, "uint16"), "LB": _s(16, "uint16"),
+    "QI": _s(8, "bfloat16"), "OH": _s(48, "bfloat16"), "BT": _s(96, "float16"), "SS": _s(48),
+    "AA": _s(384, "float16"), "AT": _s(128), "DX": _s(128), "DQ": _s(128, "bfloat16"), "XR": _s(128), "YS": _s(128),
+    "GTA": _s(80), "GTB": _s(128), "GI": _s(80, "float16"), "GD": _s(128, "float16"), "GDF": _s(128), "GSF": _s(8, "float16"), "GV1": _s(8), "HV1": _s(48),
 }
 for _t in "HG":
-    _n = 128 if _t == "H" else 80
-    SCRATCH.update({_t + "P": _s(_n), _t + "N": _s(_n, "bfloat16"), _t + "SC": _s(80), _t + "D0": _s(40), _t + "D1": _s(40),
-                    _t + "Z": _s(40), _t + "D": _s(128, "float16"), _t + "V0": _s(40 if _t == "G" else 8), _t + "V1": _s(40 if _t == "G" else 8)})
+    SCRATCH.update({_t + "P": _s(128), _t + "N": _s(128, "bfloat16"), _t + "SC": _s(80), _t + "X": _s(40), _t + "Z": _s(40), _t + "V0": _s(40)})
 for _k in range(R):
-    SCRATCH["MS%d" % _k] = _s(12, "float16")
-    SCRATCH["LM%d" % _k] = _s(10, "float16")
-    SCRATCH["RT%d" % _k] = _s(8)
+    SCRATCH["MS%d" % _k] = _s(12, "uint16")
+    SCRATCH["LM%d" % _k] = _s(10, "uint16")
+    SCRATCH["RT%d" % _k] = _s(25)
     SCRATCH["RL%d" % _k] = _s(8)
 for _k in range(8):
     SCRATCH["b%d" % _k] = ("psum", [128, 512], "float32")
 
-SEMAPHORES = ["v", "t", "s", "c", "ltet", "lpts", "lpl", "lnt", "lnd", "lnb", "sty", "pd", "sent"] + ["rq%d" % k for k in range(R)] + ["rt%d" % k for k in range(R)]
+SEMAPHORES = (["v", "t", "s", "c", "ltet", "lpts", "lpq", "lqr", "lpl", "lnt", "lnd", "sty", "pd", "sent"]
+              + ["rq%d" % k for k in range(R)] + ["rt%d" % k for k in range(R)])
 BANKS = ["b%d" % k for k in range(8)]
 
 
 def slot(owner, other):
     return other - (1 if other > owner else 0)
+
+
+def coarse(u):
+    return 1.5 * 2.0 ** 23 * u
 
 
 def engine_split(topo, src, dsts):
@@ -74,6 +73,27 @@ def engine_split(topo, src, dsts):
     return out
 
 
+def in_order(calls):
+    tail = [0.0] * len(calls)
+    for i in range(len(calls) - 1, -1, -1):
+        q, cost, delay, before = calls[i]
+        tail[i] += cost + delay
+        for b in before:
+            tail[b] = max(tail[b], tail[i])
+    start, busy = {}, {}
+    for i in sorted(range(len(calls)), key=lambda i: (-tail[i], i)):
+        q, cost, delay, before = calls[i]
+        t = max([0.0] + [start[b] + calls[b][1] + (0.0 if q == calls[b][0] in ("t", "c") else calls[b][2]) for b in before])
+        for a, e in sorted(busy.get(q, [])):
+            if t + cost <= a:
+                break
+            t = max(t, e)
+        start[i] = t
+        if q:
+            busy.setdefault(q, []).append((t, t + cost))
+    return sorted(range(len(calls)), key=lambda i: (start[i], i))
+
+
 def rank_program(g, core, T, topo):
     me = T.rank_of(core)
     if me is None:
@@ -83,6 +103,23 @@ def rank_program(g, core, T, topo):
     op = AluOpType
     act = ActivationFunctionType
     rel = float(OFF - TT * me)
+
+    calls, issue, last_w, last_r, dmas = [], [], {}, {}, {}
+
+    def note(q, cost, delay, r, w, fn, more=()):
+        before = set(more)
+        for k in r + w:
+            before.update(last_w.get(k, []))
+        for k in w:
+            before.update(last_r.get(k, []))
+        i = len(calls)
+        calls.append((q, cost, delay, sorted(before)))
+        issue.append(fn)
+        for k in r:
+            last_r.setdefault(k, []).append(i)
+        for k in w:
+            last_w[k], last_r[k] = [i], []
+        return i
 
     queues = {"v": g.vector, "t": g.tensor, "s": g.scalar, "c": g, "y": g.sync}
     known = {q: {} for q in queues}
@@ -114,418 +151,364 @@ def rank_program(g, core, T, topo):
                 continue
             wait(q, s, n)
 
-    def do(q, fn, r, w):
+    def do(q, fn, r, w, cost, after=""):
         r, w = r.split(), w.split()
-        need(q, r, w)
-        fn(queues[q]).then_inc(T.sem[q], 1)
-        count[q] += 1
-        ev = (q, count[q])
-        clocks[ev] = dict(known[q])
-        clocks[ev][q] = count[q]
-        for k in r:
-            readers.setdefault(k, []).append(ev)
-        for k in w:
-            writers[k] = [ev]
-            readers[k] = []
 
-    def event(sem, total, w):
-        clocks[(sem, total)] = {sem: total}
-        for k in w.split():
-            writers[k] = [(sem, total)]
-            readers[k] = []
+        def go():
+            need(q, r, w)
+            fn(queues[q]).then_inc(T.sem[q], 1)
+            count[q] += 1
+            ev = (q, count[q])
+            clocks[ev] = dict(known[q])
+            clocks[ev][q] = count[q]
+            for k in r:
+                readers.setdefault(k, []).append(ev)
+            for k in w:
+                writers[k] = [ev]
+                readers[k] = []
+        note(q, cost, LAT, r, w, go, [i for k in after.split() for i in last_w[k]])
 
-    def dma(q, sem, out, in_, r="", w=""):
-        need(q, r.split(), w.split())
-        queues[q].dma_start(out, in_).then_inc(T.sem[sem], 16)
+    def event(sem, total, w, delay=LOCAL):
+        def go():
+            clocks[(sem, total)] = {sem: total}
+            for k in w.split():
+                writers[k] = [(sem, total)]
+                readers[k] = []
+        note(None, 0.0, delay, [], w.split(), go, dmas[sem])
 
-    def tt(out, a, b, o, r, w):
-        do("v", lambda e: e.tensor_tensor(out=out, in0=a, in1=b, op=o), r, w)
+    def dma(q, sem, out, in_, r="", after=""):
+        def go():
+            need(q, r.split(), [])
+            queues[q].dma_start(out, in_).then_inc(T.sem[sem], 16)
+        dmas.setdefault(sem, []).append(note(q, 0.05, 0.0, r.split(), [], go, [i for s in after.split() for i in dmas[s]]))
+
+    def width(ap):
+        return ap.shape[1]
+
+    def plain(n):
+        return max(n, 64) * CYC
+
+    def picked(n):
+        return 0.06 + 1.56 * n * CYC
+
+    def tt(out, a, b, o, r, w, by=None):
+        n = width(out)
+        both = 1 if any(k in BANKS for k in r.split()) else 2
+        do("v", lambda e: e.tensor_tensor(out=out, in0=a if by is None else a.indirect(by), in1=b, op=o), r, w, plain(both * n) if by is None else picked(n))
 
     def ts(out, a, s1, o0, r, w, s2=None, o1=None):
         if o1 is None:
-            do("v", lambda e: e.tensor_scalar(out, a, s1, None, op0=o0), r, w)
+            do("v", lambda e: e.tensor_scalar(out, a, s1, None, op0=o0), r, w, plain(width(out)))
         else:
-            do("v", lambda e: e.tensor_scalar(out, a, s1, s2, op0=o0, op1=o1), r, w)
+            do("v", lambda e: e.tensor_scalar(out, a, s1, s2, op0=o0, op1=o1), r, w, plain(width(out)))
+
+    def small(out, a, u, r, w):
+        ts(out, a, coarse(u), op.add, r, w, coarse(u), op.is_equal)
 
     def cp(out, a, r, w):
-        do("v", lambda e: e.tensor_copy(out, a), r, w)
+        do("v", lambda e: e.tensor_copy(out, a), r, w, plain(width(out)))
 
     def fill(ap, x, w):
-        do("v", lambda e: e.memset(ap, x), "", w)
+        do("v", lambda e: e.memset(ap, x), "", w, plain(width(ap)))
 
-    def sc(out, a, r, w, bias=0.0, scale=1.0, f=act.Copy):
-        do("s", lambda e: e.activation(out, a, f, bias=bias, scale=scale), r, w)
+    def sc(out, a, r, w, bias=0.0, scale=1.0, f=act.Copy, by=None):
+        n = width(out)
+        do("s", lambda e: e.activation(out, a if by is None else a.indirect(by), f, bias=bias, scale=scale), r, w, plain(n) if by is None else picked(n))
 
-    def sfill(ap, n, x, w):
-        sc(ap, T.R6[:, 0:n], "R6", w, bias=x, scale=0.0)
+    def sfill(ap, x, w, at=0):
+        sc(ap, T.ON[at:at + ap.shape[0], 0:width(ap)], "ON", w, bias=float(x), scale=0.0)
 
     def scan(out, d0, d1, o0, o1, r, w):
-        do("v", lambda e: e.tensor_tensor_scan(out, d0, d1, 0.0, o0, o1), r, w)
+        do("v", lambda e: e.tensor_tensor_scan(out, d0, d1, 0.0, o0, o1), r, w, plain(width(out)))
 
-    def mm(out, lhsT, rhs, start, stop, r, w):
-        do("t", lambda e: e.matmul(out, lhsT, rhs, start, stop), r, w)
+    def mm(out, lhsT, rhs, start, stop, r, w, wide=False):
+        do("t", lambda e: e.matmul(out, lhsT, rhs, start, stop), r, w, max(min(64, out.shape[0]), width(out)) * (4 if wide else 1) * CYC)
 
-    def iota(out, pattern, base, cm, w, small=True):
-        if small:
-            do("c", lambda e: e.iota(out, pattern, base, cm, allow_small_or_imprecise_dtypes=True), "", w)
+    def iota(out, pattern, base, cm, w, whole=False, after=""):
+        if whole:
+            do("c", lambda e: e.iota(out, pattern, base, cm), "", w, 0.13 + 2 * width(out) * CYC, after)
         else:
-            do("c", lambda e: e.iota(out, pattern, base, cm), "", w)
+            do("c", lambda e: e.iota(out, pattern, base, cm, allow_small_or_imprecise_dtypes=True), "", w, 0.13 + 2 * width(out) * CYC, after)
 
     split = engine_split(topo, core, [cores[q] for q in others])
     into = sum(len(engine_split(topo, cores[q], [c for c in cores if c != cores[q]])[core]) for q in others)
     sent = [0]
 
-    def send(src, dst, sem, r):
-        need("c", r.split(), [])
-        tr = []
-        for q in others:
-            rid, pid = topo.addr(cores[q])[:2]
-            tr.append(RemoteDMATransfer(dst_ids=[DstId(rid=rid, pnc=pid)], dma_engine_mask=sum(1 << e for e in split[cores[q]]),
-                                        remote_sem=T.sem[sem], src=src(q), dst=dst(q)))
-            sent[0] += len(split[cores[q]])
-        g.remote_dma_fused(tr, local_sem=T.sem.sent)
+    def send(src, dst, sem, r, w, first=0.0, after=""):
+        def go():
+            need("c", r.split(), [])
+            tr = []
+            for q in others:
+                rid, pid = topo.addr(cores[q])[:2]
+                tr.append(RemoteDMATransfer(dst_ids=[DstId(rid=rid, pnc=pid)], dma_engine_mask=sum(1 << e for e in split[cores[q]]),
+                                            remote_sem=T.sem[sem], src=src(q), dst=dst(q)))
+                sent[0] += len(split[cores[q]])
+            g.remote_dma_fused(tr, local_sem=T.sem.sent)
+        dmas[sem] = [note("c", ISSUE + first, 0.0, r.split() + after.split(), ["net"], go)]
+        event(sem, into, w, HOP)
 
-    fill(T.P4[:, :], 0, "P4")
-    dma("y", "ltet", T.T0I[:, :], T.tet0[:, :])
-    dma("s", "lnt", T.NT[:, 0:32], T.nbr[:, :])
-    for b in range(4):
-        dma("y" if b % 2 else "s", "lpts", T.P4[32 * b:32 * b + 24, :], T.pts[:, 32 * b:32 * b + 32], "", "P4")
-    for k in range(8):
-        dma("y" if k % 2 else "s", "lpl", T.PW[16 * k:16 * k + 16, OFF:TOP], T.planes[:, :])
-
-    fill(T.R6[:, :], 1.0, "R6")
-    fill(T.ON[:, :], 1.0, "ON")
-    iota(T.CI[:, 0:1], [[0, 1]], 0, 1, "CI0", small=False)
-    iota(T.IC[:, :], [[1, 128]], 0, 0, "IC", small=False)
-    iota(T.NT[:, 32:40], [[1, 8]], TT * me, 8, "NT1", small=False)
-    iota(T.QC[:, :], [[0, 8], [1, 6]], QB, 0, "QC")
-    do("c", lambda e: e.affine_select(T.UT[:, :], T.ON[:, :], [[1, 128]], op.is_gt, 0.0, 0, -1), "ON", "UT")
-    do("c", lambda e: e.affine_select(T.UT[:, :], T.UT[:, :], [[1, 128]], op.not_equal, 256.0, 0, -1), "UT", "UT")
-    iota(T.RKI[:, :], [[4, 8], [-1, 5]], 4, 0, "RKI")
-    event("ltet", 16, "T0I")
-    event("lnt", 16, "NT0")
-    event("lpts", 64, "P4")
-    event("lpl", 128, "PWa")
-
-    fill(T.R6[:, 0::6], 0.0, "R6")
-    for ap, n, x, w in ((T.GZ[:, :], 40, 0.0, "GZ"), (T.GV0[:, :], 40, 0.0, "GV0"), (T.GV1[:, :], 40, 0.0, "GV1"), (T.R5[:, 0::2], 40, 2 * BIG, "R5"),
-                        (T.R5[:, 1::2], 40, KEY / 2, "R5"), (T.R5[:, 0::10], 8, -BIG, "R5"), (T.R5[:, 1::10], 8, -BIG - KEY, "R5"),
-                        (T.CR[:, 0::2], 40, KEY / 2, "CR"), (T.CR[:, 1::2], 40, -KEY / 2, "CR"), (T.CR[:, 0::10], 8, 2 * BIG, "CR"),
-                        (T.CR[:, 1::10], 8, BIG, "CR")):
-        sfill(ap, n, x, w)
     rs, an = op.arith_shift_right, op.bitwise_and
-    ts(T.CI[:, 1:2], T.CI[:, 0:1], 15, an, "CI0", "CI1")
-    ts(T.CI[:, 2:3], T.CI[:, 0:1], 4, rs, "CI0", "CI2")
-    ts(T.CI[:, 3:4], T.CI[:, 0:1], 2, rs, "CI0", "CI3")
-    ts(T.CI[:, 4:5], T.CI[:, 0:1], 4, rs, "CI0", "CI4", 1, an)
-    ts(T.CI[:, 5:6], T.CI[:, 0:1], 3, an, "CI0", "CI5")
-    ts(T.CI[:, 6:7], T.CI[:, 0:1], 5, rs, "CI0", "CI6")
-    ts(T.CI[:, 7:8], T.CI[:, 0:1], 31, an, "CI0", "CI7")
-    ts(T.ICM[:, :], T.IC[:, :], 15, an, "IC", "ICM")
-    cp(T.CF[:, :], T.CI[:, :], "CI0 CI1 CI2 CI3 CI4 CI5 CI6 CI7", "CF")
-    p, p15, pg, p2, podd, p3, p5, p31 = [T.CF[:, k:k + 1] for k in range(8)]
-    cp(T.LT[:, :], T.IC[:, 0:8], "IC", "LT")
-    ts(T.MI[:, :], T.ICM[:, :], p15, op.is_equal, "ICM CF", "MI")
-    ts(T.GS[:, :], T.IC[:, 0:8], pg, op.is_equal, "IC CF", "GS")
-    ts(T.NI[:, 0:3], T.IC[:, 0:3], 16.0, op.mult, "IC CF", "NI", p15, op.add)
-    ts(T.N6[:, 0:3], T.NI[:, 0:3], 1.0 / 6, op.mult, "NI", "N6", -2.5 / 6, op.add)
-    ts(T.L6[:, 0:3], T.N6[:, 0:3], 6.0, op.mult, "N6", "L6", 5.0, op.add)
+    add, sub, mult, eq, lo, hi = op.add, op.subtract, op.mult, op.is_equal, op.min, op.max
+    mine = T.PD[:, 32 * me:32 * me + 32]
 
-    cp(T.P4H[:, :], T.P4[:, :], "P4", "P4H")
-    send(lambda q: T.P4H[:, :], lambda q: T.PD[:, 32 * slot(q, me):32 * slot(q, me) + 32], "pd", "P4H")
-    event("pd", into, "PD")
-    iota(T.RNI[:, :], [[16, 8], [-1, 5]], 4, 0, "RNI")
-    iota(T.C5[:, :], [[-5, 3]], 0, 1, "C5")
-    iota(T.G48[:, :], [[1, 8], [0, 6]], 0, 0, "G48")
+    dma("y", "ltet", T.T0I[:, :], T.tet0[:, :])
+    for c in range(3):
+        dma("y" if c % 2 else "s", "lpts", T.P4[32 * c:32 * c + 32, :], T.pts[c::3, :])
+    dma("y", "lnt", T.NT[0:64, :], T.nbr[:, :])
+    for k in range(8):
+        dma("y", "lpl", T.PW[16 * k:16 * k + 16, OFF:TOP], T.planes[:, :], "", "ltet lnt lpts")
+    event("lpts", 48, "P4", 1.9)
+    event("ltet", 16, "T0I")
+    event("lnt", 16, "NT0", 1.9)
+    event("lpl", 128, "PWa", 2 * LOCAL)
 
-    def spread(bank, at, n, src, b):
-        mm(T[bank][:, at:at + n], T.SEL[32 * b:32 * b + 32, :], T[src][32 * b:32 * b + 32, :], True, True, src + " SEL", bank)
+    fill(T.ON[:, :], 1.0, "ON")
+    iota(T.NT[64:80, :], [[1, 64]], TT * me, 64, "NT1 PO", True)
+    iota(T.PO[:, :], [[-8, 4]], -7, 2, "PO")
+    iota(T.M2[:, :], [[0, 8], [2, 16]], -15, 0, "M2", after="PO")
+    iota(T.E48[:, :], [[-32, 8], [0, 6]], -15, 2, "E48", after="M2")
+    iota(T.DC[:, :], [[1, 128]], 0, -1, "DC", after="E48")
+    for k, u in ((0, 16), (1, 32)):
+        ts(T.PR[:, k:k + 1], T.PO[:, k:k + 1], coarse(u), add, "PO", "PR%d" % k, coarse(u), sub)
+    ts(T.PR[:, 3:4], T.PO[:, 3:4], coarse(64), add, "PO", "PR3", coarse(64), sub)
+    ts(T.LT[:, :], T.M2[:, 0:8], 0.5, mult, "M2", "LT", 7.5, add)
+    ts(T.LD[:, :], T.M2[:, 0:8], 2.5, mult, "M2", "LD", 41.5, add)
+    ts(T.MI[:, :], T.M2[:, :], T.PR[:, 1:2], add, "M2 PR1 PO", "MI", T.PO[:, 1:2], eq)
+    small(T.GS48[:, :], T.E48[:, :], 32, "E48", "GS48")
+    GS = T.GS48[:, 0::6]
+    sfill(T.ONF[0:1, :], 1.0, "ONF")
+    for q in range(N):
+        sfill(T.CY[0:1, q::6], -TT * q - MID, "CY%d" % q)
+    cy = " ".join("CY%d" % q for q in range(N))
+    ts(T.UT[:, :], T.DC[:, :], 0.0, eq, "DC", "UT", 256.0, mult)
+    do("c", lambda e: e.affine_select(T.UT[:, :], T.UT[:, :], [[-1, 128]], op.is_ge, 1.0, 0, 1), "UT", "UT", 0.17 + 256 * CYC)
+    sfill(T.R6[:, :], 1.0, "R6")
+    sfill(T.R6[:, 0::6], 0.0, "R6")
+    sfill(T.C26[:, :], 26.0, "C26")
+    ts(T.CX[:, 5:6], T.PR[:, 0:1], T.PO[:, 0:1], sub, "PR0 PO", "CX5", -3.0, mult)
+    ts(T.LA[:, :], T.C26[:, :], T.CX[:, 5:6], add, "C26 CX5", "LA")
+    for k in range(8):
+        sc(T.IA[:, k::8], T.M2[:, 0:16], "M2", "IA%d" % k, bias=263.5, scale=0.5)
+    ia = " ".join("IA%d" % k for k in range(8))
+    sfill(T.AA[:, 0:128], 0.0, "AA0")
+    sfill(T.AA[:, 256:384], 0.0, "AA1")
+    ts(T.CX[:, 6:7], T.PR[:, 3:4], 5.0, mult, "PR3 PO", "CX6", T.PO[:, 3:4], add)
+    ts(T.CX[:, 0:1], T.CX[:, 6:7], 0.5, mult, "CX6", "CX0", 15.5 + 32 * me - MID - OFF, add)
+    for k in range(R):
+        sfill(T["RL%d" % k][:, :], 0.0, "RL%d0" % k)
 
-    def guest_points():
-        for b, bank in enumerate(("b0", "b1", "b2", "b6")):
-            spread(bank, 0, 160, "PD", b)
-        for b, bank in ((0, "b0"), (2, "b2")):
-            sc(T.PT[:, 160 * b:160 * b + 160], T[bank][:, 0:160], bank + " CX2", "PT%d" % b, bias=T.CX[:, 2:3], f=act.Identity)
-        yield
-        for b, bank in ((1, "b1"), (3, "b6")):
-            ts(T.PT[:, 160 * b:160 * b + 160], T[bank][:, 0:160], T.CX[:, 2:3], op.add, bank + " CX2", "PT%d" % b)
-        yield
+    iota(T.KD[:, :], [[4, 8], [0, 4], [32, 4]], 0, -1, "KD", after="UT")
+    iota(T.FK[:, :], [[-32, 8], [8, 5]], -35, 2, "FK", after="KD")
+    iota(T.FB[:, :], [[-48, 8], [9, 5]], -39, 3, "FB", after="FK")
+    for ap, x, w in ((T.R5[:, 0::2], 2 * BIG, "R5"), (T.R5[:, 1::2], KEY / 2, "R5"), (T.R5[:, 0::10], -BIG, "R5"), (T.R5[:, 1::10], -BIG - KEY, "R5"),
+                     (T.CR[0:1, 0::2], KEY / 2, "CR"), (T.CR[0:1, 1::2], -KEY / 2, "CR"), (T.CR[0:1, 0::10], 2 * BIG, "CR"), (T.CR[0:1, 1::10], BIG, "CR"),
+                     (T.GZ[:, :], 0.0, "GZ"), (T.GV0[:, :], 0.0, "GV0"), (T.GV1[:, :], 0.0, "GV1"), (T.HV0[:, :], 0.0, "HV0"),
+                     (T.NW[:, 0:OFF], 0.0, "NWp0"), (T.NW[:, TOP + 1:W], 0.0, "NWp1")):
+        sfill(ap, x, w)
+    ts(T.NW[:, TOP:TOP + 1], T.MI[:, 12:13], T.MI[:, 14:15], sub, "MI", "NWp2", float(FAR), mult)
+    fill(T.LB[:, :], 0, "GLB JLB")
+    fill(T.PW[:, 0:OFF], 0, "PWb0")
+    fill(T.PW[:, TOP:W], 0, "PWb1")
+    small(T.RK1[:, :], T.FK[:, :], 8, "FK", "RK1")
+    sfill(T.RK1[:, 0::5], 0.0, "RK1")
+    sc(T.RK[:, 0::2], T.RK1[:, :], "RK1", "RKa", scale=-KEY)
+    sc(T.RK[:, 1::2], T.RK1[:, :], "RK1", "RKb", scale=KEY)
+    small(T.RN1[:, :], T.FB[:, :], 8, "FB", "RN1")
+    ts(T.RN2[:, :], T.FB[:, :], 3.0, eq, "FB", "RN2")
+    tt(T.RN0[:, :], T.RN1[:, :], T.RN2[:, :], sub, "RN1 RN2", "RN0")
+    for a, b in (("RNA", "RN0"), ("RNB", "RN1")):
+        tt(T[a][:, 0:39], T[b][:, 0:39], T[b][:, 1:40], sub, b, a)
+        sc(T[a][:, 4::5], T[b][:, 4::5], b, a)
+    ts(T.IDF[:, :], T.DC[:, :], 0.0, eq, "DC", "IDF")
+    sc(T.IDH[:, :], T.IDF[:, :], "IDF", "IDH")
+    sc(T.GSH[:, :], GS, "GS48", "GSH")
+    sc(T.GSF[:, :], GS, "GS48", "GSF")
+    sc(T.MIH[0:16, :], T.MI[0:16, :], "MI", "MIH")
 
-    def window():
-        for b in (1, 2, 0):
-            r = "NS%d" % b
-            dma("y", "lnd", T.ND[5 * b:5 * b + 4, :], T.NS[:, 40 * b:40 * b + 32], r)
-            dma("s", "lnd", T.ND[5 * b + 4:5 * b + 5, :], T.NS[:, 40 * b + 32:40 * b + 40], r)
-        dma("y", "lnd", T.ND[15:16, :], T.NS[:, 112:120], "NS2")
-        event("lnd", 7 * 16, "ND")
-        for k in range(8):
-            dma("y", "lnb", T.NW[16 * k:16 * k + 16, OFF:TOP], T.ND[:, :], "ND")
-        event("lnb", 128, "NWa")
+    iota(T.CI[:, 0:1], [[0, 1]], 0, 1, "CI0", True)
+    iota(T.IC[:, :], [[1, 128]], 0, 0, "IC", True)
+    for k, ops in enumerate(((15, an), (4, rs), (7, an), (1, an), (1, rs, 7, an))):
+        ts(T.CI[:, k + 1:k + 2], T.CI[:, 0:1], ops[0], ops[1], "CI0", "CI%d" % (k + 1), *ops[2:])
+    cp(T.CF[:, 0:6], T.CI[:, 0:6], "CI0 CI1 CI2 CI3 CI4 CI5", "CF")
+    p15, pg, p7, p1, ph = [T.CF[:, k:k + 1] for k in range(1, 6)]
+    ts(T.CX[:, 1:2], p15, 8.0, mult, "CF", "CX1", pg, add)
+    ts(T.CX[:, 2:3], p1, 8.0, mult, "CF", "CX2", pg, add)
+    ts(T.CX[:, 4:5], T.CX[:, 2:3], 2.0, mult, "CX2", "CX4", -15.0, add)
+    ts(T.CX[:, 3:4], p7, 5.0, mult, "CF", "CX3", -22.0, add)
+    ts(T.IDP[:, :], T.IC[:, :], T.CX[:, 1:2], eq, "IC CX1", "IDP")
+    sc(T.IDQ[:, :], T.IDP[:, :], "IDP", "IDQ")
+    ts(T.MIP[:, :], T.M2[:, :], T.CX[:, 4:5], eq, "M2 CX4", "MIP")
+    ts(T.GSP[:, :], T.IC[:, 0:8], ph, eq, "IC CF", "GSP")
+    ts(T.LP[:, :], T.C26[:, :], T.CX[:, 3:4], add, "C26 CX3", "LP")
+    ts(T.IC3[:, :], T.IC[:, :], 3, rs, "IC", "IC3")
+    ts(T.MI8[:, :], T.IC3[:, :], p15, eq, "IC3 CF", "MI8")
 
-    def constants():
-        fill(T.US[:, :], 0.0, "US")
-        yield
-        ts(T.NA[:, :], T.NT[:, :], 10, rs, "NT0 NT1", "NA")
-        yield
-        fill(T.QI[:, :], 0.0, "QI")
-        yield
-        ts(T.NP[:, 40:80], T.NT[:, :], 63, an, "NT0 NT1", "NP1")
-        yield
-        ts(T.NU[:, :], T.NA[:, :], float(me), op.is_equal, "NA", "NU", FAR - rel, op.mult)
-        yield
-        ts(T.NP[:, 0:40], T.NT[:, :], 8192 - 64, an, "NT0 NT1", "NP0")
-        yield
-        cp(T.NS[:, 40:80], T.NP[:, 40:80], "NP1", "NS1")
-        yield
-        ts(T.NS[:, 80:120], T.NU[:, :], float(-FAR), op.add, "NU", "NS2")
-        yield
-        ts(T.CV[:, :], T.QC[:, :], -1.0, op.mult, "QC", "CV", QB - BASE + OFF / float(TT), op.add)
-        yield
-        ts(T.CJ0[:, :], T.QC[:, :], float(QB + me), op.is_lt, "QC", "CJ0", -32.0, op.mult)
-        yield
-        tt(T.NS[:, 0:40], T.NP[:, 0:40], T.NS[:, 80:120], op.subtract, "NP0 NS2", "NS0")
-        window()
-        yield
-        ts(T.CX[:, 0:1], p5, 160.0, op.mult, "CF", "CX0", p31, op.add)
-        yield
-        ts(T.CJ[:, :], T.CJ0[:, :], T.CX[:, 0:1], op.add, "CJ0 CX0", "CJ", 32.0 * me, op.add)
-        yield
-        ts(T.LA[:, :], T.IC[:, 0:8], 6.0, op.mult, "IC", "LA", 5.0, op.add)
-        yield
-        ts(T.IA[:, :], T.ICM[:, :], 256.0, op.add, "ICM", "IA")
-        yield
-        ts(T.SA[:, :], T.IC[:, :], 4, rs, "IC", "SA")
-        yield
-        ts(T.SB[:, :], T.IC[:, :], 3, an, "IC", "SB")
-        yield
-        ts(T.SV[:, :], T.SA[:, :], 3.0, op.mult, "SA", "SV")
-        yield
-        ts(T.CX[:, 1:2], podd, -1.0, op.mult, "CF", "CX1", 1.0, op.add)
-        yield
-        tt(T.SV[:, :], T.SV[:, :], T.SB[:, :], op.add, "SV SB", "SV")
-        yield
-        fill(T.M12[:, 0::2], float(TT), "M12a")
-        yield
-        fill(T.M12[:, 1::2], 1.0, "M12b")
-        yield
-        fill(T.SV[:, 3::4], -1000.0, "SV")
-        yield
-        ts(T.MK[:, 0:12], T.M12[:, :], T.CX[:, 1:2], op.mult, "M12a M12b CX1", "MK0")
-        yield
-        ts(T.MK[:, 12:24], T.M12[:, :], podd, op.mult, "M12a M12b CF", "MK1")
-        yield
-        ts(T.SEL[:, :], T.SV[:, :], p31, op.is_equal, "SV CF", "SEL")
-        yield
-        ts(T.CX[:, 2:3], p3, 3.0, op.is_equal, "CF", "CX2")
-        for b in range(4):
-            if b:
-                wait("t", "t", count["t"])
-            spread("b3", 32 * b, 32, "P4H", b)
-        sc(T.PTH[:, :], T.b3[:, 0:128], "b3 CX2", "PTH", bias=T.CX[:, 2:3], f=act.Identity)
-        yield
-        ts(T.RK[:, 0::2], T.RKI[:, :], p2, op.is_equal, "RKI CF", "RKa", -KEY, op.mult)
-        yield
-        ts(T.RK[:, 1::2], T.RKI[:, :], p2, op.is_equal, "RKI CF", "RKb", KEY, op.mult)
-        yield
-        fill(T.RK[:, 0::10], 0.0, "RKa")
-        yield
-        fill(T.RK[:, 1::10], 0.0, "RKb")
-        yield
-        ts(T.HL[:, :], T.T0I[:, :], rel, op.add, "T0I", "HL", float(TOP), op.min)
-        yield
-        fill(T.PW[:, 0:OFF], 0, "PWb0")
-        yield
-        fill(T.PW[:, TOP:W], 0, "PWb1")
-        yield
-        fill(T.NW[:, 0:OFF], 0.0, "NWp0")
-        yield
-        fill(T.NW[:, TOP:W], 0.0, "NWp1")
-        yield
-        ts(T.IDS[:, :], T.IC[:, :], p, op.is_equal, "IC CF", "IDS", 1.0 / TT, op.mult)
-        yield
-        ts(T.RN0[:, :], T.RNI[:, :], T.C5[:, 0:1], op.is_equal, "RNI C5", "RN0")
-        yield
-        ts(T.RN1[:, :], T.RNI[:, :], T.C5[:, 1:2], op.is_equal, "RNI C5", "RN1")
-        yield
-        tt(T.RNA[:, :], T.RN0[:, :], T.RN1[:, :], op.add, "RN0 RN1", "RNA")
-        yield
-        ts(T.GSH[:, :], T.IC[:, 0:8], pg, op.is_equal, "IC CF", "GSH")
-        yield
-        ts(T.LD[:, :], T.IC[:, 0:8], 5.0, op.mult, "IC", "LD", 4.0, op.add)
-        yield
+    ts(T.NA[0:80, :], T.NT[0:80, :], 10, rs, "NT0 NT1", "NA")
+    ts(T.NP[0:80, 64:128], T.NT[0:80, :], 63, an, "NT0 NT1", "NP1")
+    ts(T.NU[0:80, :], T.NA[0:80, :], float(me), eq, "NA", "NU", FAR - rel, mult)
+    ts(T.NP[0:80, 0:64], T.NT[0:80, :], 8192 - 64, an, "NT0 NT1", "NP0")
+    cp(T.NS[0:80, 64:128], T.NP[0:80, 64:128], "NP1", "NS1")
+    ts(T.NS[0:80, 128:192], T.NU[0:80, :], float(-FAR), add, "NU", "NS2")
+    tt(T.NS[0:80, 0:64], T.NP[0:80, 0:64], T.NS[0:80, 128:192], sub, "NP0 NS2", "NS0")
+    for b in (1, 2, 0):
+        dma("y", "lnd", T.ND[b:15:3, :], T.NS[0:80, 64 * b:64 * b + 64], "NS%d" % b)
+    event("lnd", 3 * 16, "ND", 1.9)
+    for b in range(4):
+        bank = "b5" if b % 2 else "b2"
+        mm(T[bank][:, 0:256], T.MIH[0:15, :], T.ND[0:15, 256 * b:256 * b + 256], True, True, "MIH ND", bank)
+        (cp if b % 2 else sc)(T.NW[:, OFF + 256 * b:OFF + 256 * b + 256], T[bank][:, 0:256], bank, "NW%d" % b)
+    fill(T.PQ[0:96, :], 0, "PQ0")
+    for k in range(8):
+        dma("y", "lpq", T.PQ[0:96:4, 16 * k:16 * k + 16], T.pts[3 * k:3 * k + 3, :], "PQ0", "lnd")
+    event("lpq", 128, "PQ", 1.9)
 
-    def dispatch(k, more):
-        ms = "MS%d" % k
+    sfill(T.PD[96:128, 32 * me:32 * me + 32], 1.0, "PD1", 96)
+    cp(T.PD[0:96, 32 * me:32 * me + 32], T.P4[0:96, :], "P4", "PD0")
+    send(lambda q: mine, lambda q: mine, "pd", "PD0 PD1", "PD", FIRST, "NT1 E48 UT M2 PO")
+    for b in range(4):
+        ts(T.SEL[:, 128 * b:128 * b + 128], T.KD[:, :], float(-b), eq, "KD", "SEL%d" % b)
+    sfill(T.PQH[96:128, :], 1.0, "PQ1", 96)
+    cp(T.PQH[0:96, :], T.PQ[0:96, :], "PQ", "PQH")
+    mm(T.b3[:, 0:128], T.SEL[:, 0:128], T.PQH[:, :], True, True, "SEL0 PQH PQ1", "b3")
+    sc(T.HTB[:, :], T.b3[:, 0:128], "b3", "HTB")
+    for b in range(4):
+        mm(T.b4[:, 32 * b:32 * b + 32], T.SEL[:, 128 * b:128 * b + 128], mine, True, True, "SEL%d PD0 PD1" % b, "b4")
+    sc(T.HTA[:, :], T.b4[:, 0:128], "b4", "HTA")
+    for b in range(4):
+        bank, at = "b%d" % (b // 2), 192 * (b % 2)
+        mm(T[bank][:, at:at + 192], T.SEL[:, 128 * b:128 * b + 128], T.PD[:, :], True, True, "SEL%d PD PD0 PD1" % b, bank)
+        if b % 2:
+            (cp if b // 2 else sc)(T.PTA[:, 192 * b - 192:192 * b + 192], T[bank][:, 0:384], bank, "PTA%d" % (b // 2))
+    for k in range(8):
+        sfill(T.QR[:, 128 * k:128 * k + 128], 0.0, "QR%d" % k)
+    for q in others:
+        dma("s", "lqr", T.QR[4 * slot(me, q)::32, :], T.PD[:, 32 * q:32 * q + 32], "PD " + " ".join("QR%d" % k for k in range(8)))
+    event("lqr", 16 * (N - 1), "QR", 1.9)
 
-        def gap(i):
-            for _ in range(GAP[min(k, 1)][i]):
-                next(more, None)
+    def opened():
+        mm(T.b6[:, 0:48], T.ONF[0:1, :], T.CY[0:1, :], True, False, "ONF " + cy, "b6", True)
 
-        tt(T.OH[:, :], T.QI[:, :].indirect(T.L6[:, 0:3]), T.QC[:, :], op.is_equal, "QI L6 QC", "OH")
+    def slots(a, out, rhs, r, bank):
+        h = a % 2
+        at = a + 128 * (1 - h)
+        mm(out, T.AA[:, at:at + 249:8], rhs, not h, bool(h), "AA AA0 AA1 " + r, bank)
+
+    def dispatch(k):
+        ms, end = "MS%d" % k, k == R - 1
+        small(T.OH[:, :], T.b6[:, 0:48], TT, "b6", "OH")
         mm(T.b7[:, 0:48], T.UT[:, :], T.OH[:, :], True, True, "UT OH", "b7")
-        if k:
-            scan(T.US[:, :], T.R6[:, :], T.b6[:, 128:176], op.mult, op.max, "R6 b6", "US")
-        gap(0)
-        tt(T.BT[:, 1::2], T.CJ[:, :], T.OH[:, :], op.mult, "CJ OH", "BTj")
-        tt(T.VV[:, :], T.US[:, :].indirect(T.L6[:, 0:3]), T.CV[:, :], op.add, "US L6 CV", "VV")
-        scan(T.SS[:, :], T.R6[:, :], T.b7[:, 0:48], op.mult, op.max, "R6 b7", "SS")
-        gap(1)
-        tt(T.BT[:, 0::2], T.VV[:, :], T.OH[:, :], op.mult, "VV OH", "BTt")
-        tt(T.AA[:, :], T.SS[:, :].indirect(T.LA[:, 0:8]), T.IA[:, :], op.is_equal, "SS LA IA", "AA")
-        for a in range(4):
-            mm(T.b7[32 * a:32 * a + 32, 64:88], T.AA[:, 32 * a:32 * a + 32], T.BT[:, 24 * a:24 * a + 24], True, True, "AA BTj BTt", "b7")
-        gap(2)
-        tt(T.TM[:, :], T.b7[:, 64:88], T.MK[:, :], op.mult, "b7 MK0 MK1", "TM")
-        gap(3)
-        tt(T[ms][:, :], T.TM[:, 0:12], T.TM[:, 12:24], op.add, "TM", ms)
-        send(lambda q: T[ms][:, 2 * q:2 * q + 2], lambda q: T["LM%d" % k][:, 2 * slot(q, me):2 * slot(q, me) + 2], "rq%d" % k, ms)
-        event("rq%d" % k, into, "LM%d" % k)
+        tt(T.BT[:, 0::2], T.b6[:, 0:48], T.OH[:, :], mult, "b6 OH", "BTt")
+        ts(T.BT[:, 1::2], T.OH[:, :], T.CX[:, 0:1], mult, "CX0 OH", "BTj")
+        scan(T.SS[:, :], T.R6[:, :], T.b7[:, 0:48], mult, hi, "R6 b7", "SS")
+        tt(T.AA[:, 128:256], T.SS[:, :], T.IA[:, :], eq, "SS LA " + ia, "AA", T.LA[:, 0:8])
+        for a in range(8):
+            slots(a, T.b7[32 * (a // 2):32 * (a // 2) + 32, 64:76], T.BT[:, 12 * a:12 * a + 12], "BTj BTt", "b7")
+        ts(T[ms][:, :], T.b7[:, 64:76], MID + OFF, add, "b7", ms)
+        send(lambda q: T[ms][:, 2 * q:2 * q + 2], lambda q: T["LM%d" % k][:, 2 * slot(q, me):2 * slot(q, me) + 2], "rq%d" % k, ms + " RL%d0" % k, "LM%d" % k)
+        ts(T.HL[:, :], T.b6[:, me:48:6], MID + OFF, add, "b6", "HL", float(TOP), lo)
+        sc(T.QI[:, :], T.b6[:, 0:48:6], "b6", "QI", bias=QB, scale=1.0 / TT)
+        tt(T.DQ[:, :], T.QI[:, :], T["MIP" if end else "MI"][:, :], mult, "QI LT MI MIP" if end else "QI LT MI", "DQ", T.LT[:, 0:8])
+        mm(T.b5[:, 0:8], T.DQ[:, :], T["GSP" if end else "GSH"][:, :], True, True, "DQ GSH GSP" if end else "DQ GSH", "b5")
+        ts(T.LI[:, :], T.b5[:, 0:8], -QB, add, "b5", "LI")
+        ident = "IDQ" if end else "IDH"
+        for a in range(8):
+            slots(a, T.b5[32 * (a // 2):32 * (a // 2) + 32, 0:128], T[ident][:, :], ident, "b5")
+        sc(T.AT[:, :], T.b5[:, 0:128], "b5", "AT")
 
-    def hold():
-        ts(T.CHB[:, :], T.OH[:, :], HOLD, op.mult, "OH", "CHB", TT * BASE - HOLD, op.add)
-
-    def turn():
-        mm(T.b6[:, 0:128], T.AA[:, :], T.IDH[:, :], True, True, "AA IDH", "b6")
-        sc(T.AT[:, :], T.b6[:, 0:128], "b6", "AT")
-
-    def step(h, i):
+    def step(h, i, lst, ln, pt, n, m, kept=False, turned=False, z=None):
         last = i == S - 1
-        n, lst, pt, bk, bn, bc = (128, T.HL[:, 0:8], "PTH", "b3", "b4", "b5") if h == "H" else (80, T.GL[:, 0:5], "GT", "b0", "b1", "b2")
-        ln, m = h + "L", n // 16
+        bk, bn = ("b3", "b4") if h == "H" else ("b0", "b1")
         X = lambda a: T[h + a]
-        ones = lambda: mm(T[bk][0:n, 0:80], T.ON[0:1, 0:n], T.CR[0:1, :], True, False, "ON CR", bk)
-        left = lambda j: mm(T[bn][0:n, 0:40], T.IDS[0:n, 0:n], X("V%d" % j)[0:n, :], not j, False, "IDS " + h + "V%d" % j, bn)
-        if not i:
-            ones()
-        sc(X("N")[:, :], T.NW[:, :].indirect(lst), "NWp0 NWp1 NWa " + ln, h + "N")
-        tt(X("P")[:, :], T.PW[:, :].indirect(lst), T[pt][:, 0:n], op.mult, "PWa PWb0 PWb1 " + ln + " " + pt, h + "P")
-        mm(T[bk][0:n, 0:80], X("P")[:, :], T.RK[:, :], False, True, h + "P RKa RKb", bk)
-        if last:
-            mm(T[bn][0:n, 0:40], X("N")[:, :], T.RNB[:, :], h == "H", True, h + "N RNB", bn)
-        else:
-            mm(T[bn][0:n, 0:40], X("N")[:, :], T.RNA[:, :], True, True, h + "N RNA", bn)
-        yield
-        scan(X("SC")[0:n, :], T.R5[0:n, :], T[bk][0:n, 0:80], op.min, op.add, "R5 " + bk, h + "SC")
-        if h == "G":
-            sc(X("D0")[0:n, :], X("SC")[0:n, 0::2], h + "SC", h + "D0", scale=-1.0)
-        if not last:
-            ones()
-        yield
-        tt(X("D1")[0:n, :], X("SC")[0:n, 0::2], T[bn][0:n, 0:40], op.min, h + "SC " + bn, h + "D1")
-        if h == "H":
-            ts(X("D0")[0:n, :], X("SC")[0:n, 0::2], -1.0, op.mult, h + "SC", h + "D0")
-        if h == "G" and i == S - 2:
-            left(0)
-        yield
-        if h == "H" and i:
-            tt(T.CHB[:, me::6], T.CHB[:, me::6], T["HV%d" % (i - 1)][:, :], op.add, "CHB HV%d" % (i - 1), "CHB")
-        scan(X("Z")[0:n, :], X("D0")[0:n, :], X("D1")[0:n, :], op.min, op.max, h + "D0 " + h + "D1", h + "Z")
-        yield
-        if not last:
-            v, c = (T["HV%d" % i][:, :], 1) if h == "H" else (T["GV%d" % i][0:n, 0::5], TT)
-            sc(v, X("Z")[0:n, 4::5], h + "Z", h + "V%d" % i, bias=float(-FAR * c), scale=float(c), f=act.Relu)
-            tt(X("D")[:, :], X("Z")[:, :].indirect(T.LD[:, 0:8]), T.MI[:, :], op.mult, h + "Z LD MI", h + "D")
-            mm(T[bc][:, 0:m], X("D")[0:n, :], T.GSH[0:n, 0:m], True, True, h + "D GSH", bc)
-            if h == "G" and i == S - 2:
-                left(1)
-            yield
-            ts(lst, T[bc][:, 0:m], float(TOP), op.min, bc, ln)
-            yield
-        elif h == "H":
-            tt(T.CHB[:, me::6], T.CHB[:, me::6], T.HZ[:, 4::5], op.add, "CHB HZ", "CHB")
-            yield
-        else:
-            tt(T.GDF[:, :], T.GZ[:, :].indirect(T.LD[:, 0:8]), T.MI[:, :], op.mult, "GZ LD MI", "GDF")
-            mm(T[bc][:, 0:m], T.GDF[0:n, :], T.GS[0:n, 0:m], True, True, "GDF GS", bc)
-            yield
+        mm(T[bk][0:n, 0:10 * m], T.ON[0:1, 0:n], T.CR[0:1, 0:10 * m], True, False, "ON CR", bk)
+        if kept:
+            mm(T[bn][0:n, 0:5 * m], T.IDF[0:n, 0:n], X("V0")[0:n, 0:5 * m], True, False, "IDF " + h + "V0", bn, True)
+        sc(X("N")[:, 0:n], T.NW[:, :], "NWp0 NWp1 NWp2 NW0 NW1 NW2 NW3 " + ln, h + "N", by=lst)
+        tt(X("P")[:, 0:n], T.PW[:, :], T[pt][:, 0:n], mult, "PWa PWb0 PWb1 " + ln + " " + pt, h + "P", lst)
+        mm(T[bk][0:n, 0:10 * m], X("P")[0:16 * m, 0:n], T.RK[0:16 * m, 0:10 * m], False, True, h + "P RKa RKb", bk, True)
+        rn = "RNB" if last else "RNA"
+        mm(T[bn][0:n, 0:5 * m], X("N")[0:16 * m, 0:n], T[rn][0:16 * m, 0:5 * m], not kept, not turned, h + "N " + rn, bn)
+        if turned:
+            mm(T[bn][0:n, 0:25:5], T.GDF[0:80, :], T.GS48[0:80, 0:30:6], False, True, "GDF GS48", bn, True)
+        scan(X("SC")[0:n, 0:10 * m], T.R5[0:n, 0:10 * m], T[bk][0:n, 0:10 * m], lo, add, "R5 " + bk, h + "SC")
+        ts(X("X")[0:n, 0:5 * m], X("SC")[0:n, 0:10 * m:2], 0.0, op.is_lt, h + "SC", h + "X")
+        z = z or h + "Z"
+        scan(T[z][0:n, 0:5 * m], X("X")[0:n, 0:5 * m], T[bn][0:n, 0:5 * m], mult, add, h + "X " + bn, z)
+        return T[z][0:n, 4:5 * m:5]
+
+    def left(out, z, r, w):
+        sc(out, z, r, w, bias=float(-FAR), f=act.Relu)
 
     def home(k):
-        if k:
-            to_list()
-            yield
-            hold()
-            turn()
-            yield
-            ts(T.HL[:, :], T.b5[:, 0:8], rel - TT * BASE, op.add, "b5", "HL", float(TOP), op.min)
-            yield
-        for i in range(S):
-            for _ in step("H", i):
-                yield
+        hl = T.HL[:, 0:8]
+        z = step("H", 0, hl, "HL", "HTB", 128, 8)
+        ts(hl, z, float(TOP), lo, "HZ", "HL")
+        left(T.HV0[:, 0::5], z, "HZ", "HV0")
+        z = step("H", 1, hl, "HL", "HTA", 128, 8)
+        ts(hl, z, float(TOP), lo, "HZ", "HL")
+        if k < R - 1:
+            for q in range(N):
+                left(T.HV1[:, q::6], z, "HZ", "HV1%d" % q)
+            opened()
+            mm(T.b6[:, 0:48], T.IDF[:, :], T.HV1[:, :], False, False, "IDF " + " ".join("HV1%d" % q for q in range(N)), "b6", True)
+        else:
+            left(T.HV1[:, 0::6], z, "HZ", "HV10")
+            mm(T.b6[0:8, 0:128], T.HV1[:, 0::6], T.IDP[:, :], True, False, "IDP HV10", "b6", True)
+        step("H", 2, hl, "HL", "HTB", 128, 8, kept=True)
+        if k < R - 1:
+            tt(T.DX[:, :], T.HZ[:, :], T.MI[:, :], mult, "HZ LD MI", "DX", T.LD[:, 0:8])
+            mm(T.b6[:, 0:48], T.DX[:, :], T.GS48[:, :], False, False, "DX GS48", "b6", True)
+        else:
+            tt(T.DX[:, :], T.HZ[:, :], T.MI8[:, :], mult, "HZ LP MI8", "DX", T.LP[:, 0:8])
+            mm(T.b6[0:8, 0:128], GS, T.DX[:, :], False, False, "DX GS48", "b6", True)
 
-    def guests(k, own):
-        lm = "LM%d" % k
-        cp(T.JL[:, 0:5], T[lm][:, 1::2], lm, "JL")
-        sc(T.GT[:, :], T.PT[:, :].indirect(T.JL[:, 0:5]), "PT0 PT1 PT2 PT3 JL", "GT")
-        cp(T.GL[:, 0:5], T[lm][:, 0::2], lm, "GL")
-        for i in range(S):
-            mine = step("G", i)
-            for pieces in MIX[min(k, 1)][i]:
-                next(mine, None)
-                for _ in range(pieces):
-                    next(own, None)
-            for _ in mine:
-                pass
-        cp(T["RT%d" % k][:, 0:5], T.b2[:, 0:5], "b2", "RT%d" % k)
-        send(lambda q: T["RT%d" % k][:, slot(me, q):slot(me, q) + 1], lambda q: T["RL%d" % k][:, slot(q, me):slot(q, me) + 1], "rt%d" % k, "RT%d" % k)
-        event("rt%d" % k, into, "RL%d" % k)
+    def guests(k):
+        lm, rt = "LM%d" % k, "RT%d" % k
+        ja, ga = T.JLA[:, 0:5], T.GLA[:, 0:5]
+        cp(ja, T[lm][:, 1::2], lm, "JLA")
+        sc(T.GTA[:, :], T.PTA[:, :], "PTA0 PTA1 JLA", "GTA", by=ja)
+        cp(ga, T[lm][:, 0::2], lm, "GLA")
+        sc(T.GI[:, :], T.IW[:, :], "IW JLA", "GI", by=ja)
+        mm(T.b2[0:80, 0:8], T.GI[:, :], T.IDH[:, 0::16], True, True, "GI IDH", "b2")
+        cp(T.LB[0:80, 8:16], T.b2[0:80, 0:8], "b2", "JLB")
+        sc(T.GTB[:, :], T.PTB[:, :], "PTB0 PTB1 PTB2 PTB3 JLB", "GTB", by=T.LB[:, 8:16])
+        z = step("G", 0, ga, "GLA", "GTA", 80, 8)
+        tt(T.GD[:, :], T.GZ[:, :], T.MI[:, :], mult, "GZ LD MI", "GD", T.LD[:, 0:8])
+        left(T.GV0[0:80, 0::5], z, "GZ", "GV0")
+        mm(T.b2[:, 0:5], T.GD[0:80, :], T.GSF[0:80, 0:5], True, True, "GD GSF", "b2")
+        ts(ga, T.b2[:, 0:5], float(TOP), lo, "b2", "GLA")
+        z = step("G", 1, ga, "GLA", "GTA", 80, 8, kept=True)
+        ts(T.LB[0:80, 0:8], z, float(TOP), lo, "GZ", "GLB")
+        left(T.GV1[0:80, :], z, "GZ", "GV1")
+        tt(T.GDF[:, :], T.GV1[:, :], T.MI[:, :], mult, "GV1 LT MI", "GDF", T.LT[:, 0:8])
+        step("G", 2, T.LB[:, 0:8], "GLB", "GTB", 128, 5, turned=True, z=rt)
+        send(lambda q: T[rt][:, 5 * slot(me, q) + 4:5 * slot(me, q) + 5], lambda q: T["RL%d" % k][:, me:me + 1], "rt%d" % k, rt, "RL%d" % k)
 
     def replies(k):
-        mm(T.b6[:, 128:176], T.IDS[:, :], T.CHB[:, :], True, False, "IDS CHB", "b6")
-        tt(T.RX[:, :], T["RL%d" % k][:, 0:5].indirect(T.LR[:, 0:3]), T.M48[:, :], op.mult, "RL%d LR M48" % k, "RX")
-        mm(T.b6[:, 128:176], T.AT[:, :], T.RX[:, :], False, True, "AT RX", "b6")
+        tt(T.XR[:, :], T["RL%d" % k][:, :], T.AT[:, :], mult, "RL%d RL%d0 LI AT" % (k, k), "XR", T.LI[:, 0:8])
         if k < R - 1:
-            scan(T.QI[:, :], T.R6[:, :], T.b6[:, 128:176], op.mult, op.max, "R6 b6", "QI")
+            mm(T.b6[:, 0:48], T.XR[:, :], T.GS48[:, :], False, True, "XR GS48", "b6", True)
         else:
-            scan(T.US[:, :], T.R6[:, :], T.b6[:, 128:176], op.mult, op.max, "R6 b6", "US")
+            mm(T.b6[0:8, 0:128], GS, T.XR[:, :], False, True, "XR GS48", "b6", True)
 
-    def to_list():
-        tt(T.DX[:, :], T.US[:, :].indirect(T.LA[:, 0:8]), T.MI[:, :], op.mult, "US LA MI", "DX")
-        mm(T.b5[:, 0:8], T.DX[:, :], T.GSL[:, :], True, True, "DX GSL", "b5")
-
-    tt(T.DX[:, :], T.T0I[:, :].indirect(T.LT[:, 0:8]), T.MI[:, :], op.mult, "T0I LT MI", "DX")
-    mm(T.b7[:, 0:8], T.DX[:, :], T.GS[:, :], True, True, "DX GS", "b7")
-    first = constants()
-    for _ in range(GAP0[0]):
-        next(first)
-    ts(T.QI[:, 5::6], T.b7[:, 0:8], 1.0 / TT, op.mult, "b7", "QI", BASE, op.add)
-    for _ in range(GAP0[1]):
-        next(first)
-    ts(T.US[:, 5::6], T.b7[:, 0:8], 1.0 / TT, op.mult, "b7", "US", BASE, op.add)
-    dispatch(0, first)
-    for _ in first:
-        pass
-    ts(T.RN2[:, :], T.RNI[:, :], T.C5[:, 2:3], op.is_equal, "RNI C5", "RN2")
-    tt(T.RNB[:, :], T.RNA[:, :], T.RN2[:, :], op.add, "RNA RN2", "RNB")
-    ts(T.IDH[:, :], T.IC[:, :], p, op.is_equal, "IC CF", "IDH")
-    hold()
-    turn()
-
-    own, points = home(0), guest_points()
-    next(points)
+    opened()
+    tt(T.DX[:, :], T.T0I[:, :], T.MI[:, :], mult, "T0I LT MI", "DX", T.LT[:, 0:8])
+    mm(T.b6[:, 0:48], T.DX[:, :], T.GS48[:, :], False, True, "DX GS48", "b6", True)
     for k in range(R):
-        for i in range(PRE[min(k, 1)]):
-            next(own, None)
-            next(points, None)
-        guests(k, own)
+        dispatch(k)
         if k == 0:
-            ts(T.M48[:, :], T.G48[:, :], pg, op.is_equal, "G48 CF", "M48", 1.0 / TT, op.mult)
-            fill(T.M48[:, me::6], 0.0, "M48")
-            ts(T.N6F[:, 0:3], T.N6[:, 0:3], -6.0, op.mult, "N6", "N6F")
-            tt(T.NM[:, 0:3], T.NI[:, 0:3], T.N6F[:, 0:3], op.add, "NI N6F", "NM")
-            ts(T.NG[:, 0:3], T.NM[:, 0:3], float(me), op.is_gt, "NM", "NG")
-            tt(T.NK[:, 0:3], T.NM[:, 0:3], T.NG[:, 0:3], op.subtract, "NM NG", "NK")
-            ts(T.LR[:, 0:3], T.NK[:, 0:3], 4.0, op.min, "NK", "LR")
-            ts(T.GSL[:, :], T.GS[:, :], float(TT), op.mult, "GS", "GSL")
-        for _ in own:
-            pass
+            iota(T.IW[:, :], [[32, 4], [0, 6], [1, 32]], 0, 8, "IW", after="net FB")
+            for b in range(4):
+                bank = T["b7" if b % 2 else "b6"][:, 0:256]
+                mm(bank, T.SEL[:, 0:128], T.QR[:, 256 * b:256 * b + 256], True, True, "SEL0 QR", "b7" if b % 2 else "b6")
+                sc(T.PTB[:, 256 * b:256 * b + 256], bank, "b7" if b % 2 else "b6", "PTB%d" % b)
+        guests(k)
+        home(k)
         replies(k)
-        if k < R - 1:
-            own = home(k + 1)
-            dispatch(k + 1, own)
+    cp(T.YS[0:8, :], T.b6[0:8, 0:128], "b6", "YS")
+    dma("y", "sty", T.y[:, :], T.YS[0:8, :], "YS")
 
-    to_list()
-    ts(T.YS[:, :], T.b5[:, 0:8], -TT * BASE, op.add, "b5", "YS")
-    dma("y", "sty", T.y[:, :], T.YS[:, :], "YS")
+    for i in in_order(calls):
+        issue[i]()
 
     g.wait_ge(T.sem.sty, 16)
     g.wait_ge(T.sem.sent, sent[0])

@@ -6,8 +6,7 @@ OFF = 64
 TOP = TT + OFF
 W = TOP + 8
 FAR = 2048
-KEY = 16384.0
-BIG = 2.0 ** 37
+BIG = 2.0 ** 30
 MID = 511.5
 QB = 129.0
 CYC = 1.04e-3
@@ -22,31 +21,31 @@ SCRATCH = {
     "PW": _s(W, "int32"), "NW": _s(W, "bfloat16"), "T0I": _s(8, "int32"),
     "NT": _s(64, "int32"), "NA": _s(64, "int32"), "NU": _s(64), "NP": _s(128, "int32"), "NS": _s(192, "bfloat16"),
     "ND": _s(TT, "bfloat16"), "MIH": _s(128, "bfloat16"),
-    "P4": _s(32, "int32"), "PD": _s(192, "float16"), "PTA": _s(768), "PTB": _s(1024), "QR": _s(1024, "float16"),
-    "PQ": _s(128, "int32"), "PQH": _s(128, "float16"), "HTA": _s(128), "HTB": _s(128), "IW": _s(768),
-    "PO": _s(4), "PR": _s(4), "CX": _s(8), "DC": _s(128), "M2": _s(128), "E48": _s(48), "KD": _s(128), "FK": _s(40), "FB": _s(40), "C26": _s(8),
-    "CI": _s(10, "int32"), "CF": _s(10), "IC": _s(128, "int32"), "IC3": _s(128, "int32"), "SEL": _s(512, "float16"),
+    "P3": _s(128, "int32"), "PH": _s(128, "float16"), "PQ": _s(128, "int32"), "PQH": _s(128, "float16"), "HTA": _s(128), "HTB": _s(128),
+    "PO": _s(4), "PR": _s(4), "CX": _s(8), "DC": _s(128), "M2": _s(128), "E48": _s(48), "FK": _s(40), "FB": _s(40), "F5": _s(40), "C26": _s(8),
+    "KX": _s(144), "KB": _s(128), "SX": _s(144, "float16"), "SB": _s(128, "float16"), "SC": _s(132, "float16"),
+    "CI": _s(10, "int32"), "CF": _s(10), "IC": _s(128, "int32"), "IC3": _s(128, "int32"),
     "MI": _s(128), "MIP": _s(128), "MI8": _s(128), "IA": _s(128), "IDF": _s(128), "IDH": _s(128, "float16"), "IDP": _s(128), "IDQ": _s(128, "float16"),
-    "UT": _s(128, "bfloat16"), "GSH": _s(8, "bfloat16"), "GSP": _s(8, "bfloat16"), "GS48": _s(48), "CY": _s(48), "ONF": _s(128),
-    "RK1": _s(40), "RK": _s(80), "RN0": _s(40), "RN1": _s(40), "RN2": _s(40), "RNA": _s(40, "bfloat16"), "RNB": _s(40, "bfloat16"),
-    "CR": _s(80, "bfloat16"), "ON": _s(128, "bfloat16"), "R5": _s(80), "R6": _s(48),
-    "LA": _s(8, "uint16"), "LD": _s(8, "uint16"), "LT": _s(8, "uint16"), "LP": _s(8, "uint16"), "LI": _s(8, "uint16"),
-    "HL": _s(8, "uint16"), "GLA": _s(8, "uint16"), "JLA": _s(8, "uint16"), "LB": _s(16, "uint16"),
-    "QI": _s(8, "bfloat16"), "OH": _s(48, "bfloat16"), "BT": _s(96, "float16"), "SS": _s(48),
+    "UT": _s(128, "bfloat16"), "GSH": _s(8, "bfloat16"), "GSP": _s(8, "bfloat16"), "GSF": _s(8, "float16"), "GS48": _s(48), "CY": _s(48), "ONF": _s(128),
+    "RK": _s(40), "RN0": _s(40), "RN1": _s(40), "RN2": _s(40), "RNA": _s(40, "bfloat16"), "RNB": _s(40, "bfloat16"),
+    "ON": _s(132, "bfloat16"), "R5": _s(40), "R6": _s(48),
+    "LA": _s(8, "uint16"), "L5": _s(40, "uint16"), "LT": _s(8, "uint16"), "LP": _s(8, "uint16"), "LI": _s(8, "uint16"), "LE": _s(8, "uint16"),
+    "HL": _s(8, "uint16"), "GLA": _s(8, "uint16"), "GLB": _s(8, "uint16"),
+    "QI": _s(8, "bfloat16"), "OH": _s(48, "bfloat16"), "BT": _s(192, "float16"), "SS": _s(48),
     "AA": _s(384, "float16"), "AT": _s(128), "DX": _s(128), "DQ": _s(128, "bfloat16"), "XR": _s(128), "YS": _s(128),
-    "GTA": _s(80), "GTB": _s(128), "GI": _s(80, "float16"), "GD": _s(128, "float16"), "GDF": _s(128), "GSF": _s(8, "float16"), "GV1": _s(8), "HV1": _s(48),
+    "GTA": _s(80), "GTB": _s(128), "GE": _s(80, "float16"), "GY": _s(240, "float16"), "GD": _s(80, "float16"), "GDF": _s(128), "GV1": _s(8), "HV1": _s(48),
 }
 for _t in "HG":
-    SCRATCH.update({_t + "P": _s(128), _t + "N": _s(128, "bfloat16"), _t + "SC": _s(80), _t + "X": _s(40), _t + "Z": _s(40), _t + "V0": _s(40)})
+    SCRATCH.update({_t + "P": _s(128), _t + "N": _s(128, "bfloat16"), _t + "S": _s(40), _t + "X": _s(40), _t + "Z": _s(40), _t + "V0": _s(40)})
 for _k in range(R):
-    SCRATCH["MS%d" % _k] = _s(12, "uint16")
-    SCRATCH["LM%d" % _k] = _s(10, "uint16")
+    SCRATCH["MS%d" % _k] = _s(24)
+    SCRATCH["LM%d" % _k] = _s(24)
     SCRATCH["RT%d" % _k] = _s(25)
     SCRATCH["RL%d" % _k] = _s(8)
 for _k in range(8):
     SCRATCH["b%d" % _k] = ("psum", [128, 512], "float32")
 
-SEMAPHORES = (["v", "t", "s", "c", "ltet", "lpts", "lpq", "lqr", "lpl", "lnt", "lnd", "sty", "pd", "sent"]
+SEMAPHORES = (["v", "t", "s", "c", "ltet", "lpts", "lpq", "lpl", "lnt", "lnd", "sty", "sent"]
               + ["rq%d" % k for k in range(R)] + ["rt%d" % k for k in range(R)])
 BANKS = ["b%d" % k for k in range(8)]
 
@@ -215,11 +214,11 @@ def rank_program(g, core, T, topo):
         n = width(out)
         do("s", lambda e: e.activation(out, a if by is None else a.indirect(by), f, bias=bias, scale=scale), r, w, plain(n) if by is None else picked(n))
 
-    def sfill(ap, x, w, at=0):
-        sc(ap, T.ON[at:at + ap.shape[0], 0:width(ap)], "ON", w, bias=float(x), scale=0.0)
+    def sfill(ap, x, w):
+        sc(ap, T.ON[0:ap.shape[0], 0:width(ap)], "ON", w, bias=float(x), scale=0.0)
 
-    def scan(out, d0, d1, o0, o1, r, w):
-        do("v", lambda e: e.tensor_tensor_scan(out, d0, d1, 0.0, o0, o1), r, w, plain(width(out)))
+    def scan(out, d0, d1, first, o0, o1, r, w):
+        do("v", lambda e: e.tensor_tensor_scan(out, d0, d1, first, o0, o1), r, w, plain(width(out)))
 
     def mm(out, lhsT, rhs, start, stop, r, w, wide=False):
         do("t", lambda e: e.matmul(out, lhsT, rhs, start, stop), r, w, max(min(64, out.shape[0]), width(out)) * (4 if wide else 1) * CYC)
@@ -234,7 +233,7 @@ def rank_program(g, core, T, topo):
     into = sum(len(engine_split(topo, cores[q], [c for c in cores if c != cores[q]])[core]) for q in others)
     sent = [0]
 
-    def send(src, dst, sem, r, w, first=0.0, after=""):
+    def send(src, dst, sem, r, w, first=0.0):
         def go():
             need("c", r.split(), [])
             tr = []
@@ -244,75 +243,80 @@ def rank_program(g, core, T, topo):
                                             remote_sem=T.sem[sem], src=src(q), dst=dst(q)))
                 sent[0] += len(split[cores[q]])
             g.remote_dma_fused(tr, local_sem=T.sem.sent)
-        dmas[sem] = [note("c", ISSUE + first, 0.0, r.split() + after.split(), ["net"], go)]
+        dmas[sem] = [note("c", ISSUE + first, 0.0, r.split(), ["net"], go)]
         event(sem, into, w, HOP)
 
     rs, an = op.arith_shift_right, op.bitwise_and
     add, sub, mult, eq, lo, hi = op.add, op.subtract, op.mult, op.is_equal, op.min, op.max
-    mine = T.PD[:, 32 * me:32 * me + 32]
 
     dma("y", "ltet", T.T0I[:, :], T.tet0[:, :])
     for c in range(3):
-        dma("y" if c % 2 else "s", "lpts", T.P4[32 * c:32 * c + 32, :], T.pts[c::3, :])
-    dma("y", "lnt", T.NT[0:64, :], T.nbr[:, :])
+        dma("y" if c % 2 else "s", "lpts", T.P3[8 * c:8 * c + 8, :], T.pts[c::3, :])
+    dma("y", "lnt", T.NT[16:80, :], T.nbr[:, :])
     for k in range(8):
         dma("y", "lpl", T.PW[16 * k:16 * k + 16, OFF:TOP], T.planes[:, :], "", "ltet lnt lpts")
-    event("lpts", 48, "P4", 1.9)
+    event("lpts", 48, "P3", 1.8)
     event("ltet", 16, "T0I")
     event("lnt", 16, "NT0", 1.9)
     event("lpl", 128, "PWa", 2 * LOCAL)
 
     fill(T.ON[:, :], 1.0, "ON")
-    iota(T.NT[64:80, :], [[1, 64]], TT * me, 64, "NT1 PO", True)
-    iota(T.PO[:, :], [[-8, 4]], -7, 2, "PO")
+    iota(T.PO[:, :], [[-4, 4]], -3, 2, "PO")
     iota(T.M2[:, :], [[0, 8], [2, 16]], -15, 0, "M2", after="PO")
     iota(T.E48[:, :], [[-32, 8], [0, 6]], -15, 2, "E48", after="M2")
     iota(T.DC[:, :], [[1, 128]], 0, -1, "DC", after="E48")
-    for k, u in ((0, 16), (1, 32)):
+    iota(T.NT[0:16, :], [[1, 64]], TT * me, 64, "NT1", True, after="DC")
+    iota(T.KX[:, :], [[8, 3], [1, 8], [0, 6]], 0, -1, "KX", after="NT1")
+    for k, u in ((0, 8), (1, 16), (3, 32)):
         ts(T.PR[:, k:k + 1], T.PO[:, k:k + 1], coarse(u), add, "PO", "PR%d" % k, coarse(u), sub)
-    ts(T.PR[:, 3:4], T.PO[:, 3:4], coarse(64), add, "PO", "PR3", coarse(64), sub)
     ts(T.LT[:, :], T.M2[:, 0:8], 0.5, mult, "M2", "LT", 7.5, add)
-    ts(T.LD[:, :], T.M2[:, 0:8], 2.5, mult, "M2", "LD", 41.5, add)
-    ts(T.MI[:, :], T.M2[:, :], T.PR[:, 1:2], add, "M2 PR1 PO", "MI", T.PO[:, 1:2], eq)
+    ts(T.MI[:, :], T.M2[:, :], T.PR[:, 3:4], add, "M2 PR3 PO", "MI", T.PO[:, 3:4], eq)
     small(T.GS48[:, :], T.E48[:, :], 32, "E48", "GS48")
     GS = T.GS48[:, 0::6]
     sfill(T.ONF[0:1, :], 1.0, "ONF")
     for q in range(N):
-        sfill(T.CY[0:1, q::6], -TT * q - MID, "CY%d" % q)
+        fill(T.CY[0:1, q::6], -TT * q - MID, "CY%d" % q)
     cy = " ".join("CY%d" % q for q in range(N))
-    ts(T.UT[:, :], T.DC[:, :], 0.0, eq, "DC", "UT", 256.0, mult)
-    do("c", lambda e: e.affine_select(T.UT[:, :], T.UT[:, :], [[-1, 128]], op.is_ge, 1.0, 0, 1), "UT", "UT", 0.17 + 256 * CYC)
+    ts(T.UT[:, :], T.DC[:, :], 0.0, eq, "DC", "UT", 4096.0, mult)
+    do("c", lambda e: e.affine_select(T.UT[:, :], T.UT[:, :], [[-1, 128]], op.is_ge, 16.0, 0, 1), "UT", "UT", 0.17 + 256 * CYC, "KX")
     sfill(T.R6[:, :], 1.0, "R6")
     sfill(T.R6[:, 0::6], 0.0, "R6")
     sfill(T.C26[:, :], 26.0, "C26")
-    ts(T.CX[:, 5:6], T.PR[:, 0:1], T.PO[:, 0:1], sub, "PR0 PO", "CX5", -3.0, mult)
+    ts(T.CX[:, 5:6], T.PR[:, 1:2], T.PO[:, 1:2], sub, "PR1 PO", "CX5", -3.0, mult)
     ts(T.LA[:, :], T.C26[:, :], T.CX[:, 5:6], add, "C26 CX5", "LA")
-    for k in range(8):
-        sc(T.IA[:, k::8], T.M2[:, 0:16], "M2", "IA%d" % k, bias=263.5, scale=0.5)
-    ia = " ".join("IA%d" % k for k in range(8))
+    ts(T.IA[:, :], T.DC[:, :], 2.0, mult, "DC PO", "IA", T.PO[:, 1:2], add)
+    ts(T.IA[:, :], T.IA[:, :], coarse(16), add, "IA", "IA", coarse(16) - 4096, sub)
     sfill(T.AA[:, 0:128], 0.0, "AA0")
     sfill(T.AA[:, 256:384], 0.0, "AA1")
-    ts(T.CX[:, 6:7], T.PR[:, 3:4], 5.0, mult, "PR3 PO", "CX6", T.PO[:, 3:4], add)
-    ts(T.CX[:, 0:1], T.CX[:, 6:7], 0.5, mult, "CX6", "CX0", 15.5 + 32 * me - MID - OFF, add)
     for k in range(R):
         sfill(T["RL%d" % k][:, :], 0.0, "RL%d0" % k)
+        sfill(T["LM%d" % k][:, 0:4], 1.0, "LM%d0" % k)
+    ts(T.SX[0:32, :], T.KX[0:32, :], 0.0, eq, "KX", "SX")
+    cp(T.PH[0:24, :], T.P3[0:24, :], "P3", "PH")
+    mm(T.b1[:, 256:400], T.PH[0:24, :], T.SX[0:24, :], True, True, "PH SX", "b1")
 
-    iota(T.KD[:, :], [[4, 8], [0, 4], [32, 4]], 0, -1, "KD", after="UT")
-    iota(T.FK[:, :], [[-32, 8], [8, 5]], -35, 2, "FK", after="KD")
-    iota(T.FB[:, :], [[-48, 8], [9, 5]], -39, 3, "FB", after="FK")
-    for ap, x, w in ((T.R5[:, 0::2], 2 * BIG, "R5"), (T.R5[:, 1::2], KEY / 2, "R5"), (T.R5[:, 0::10], -BIG, "R5"), (T.R5[:, 1::10], -BIG - KEY, "R5"),
-                     (T.CR[0:1, 0::2], KEY / 2, "CR"), (T.CR[0:1, 1::2], -KEY / 2, "CR"), (T.CR[0:1, 0::10], 2 * BIG, "CR"), (T.CR[0:1, 1::10], BIG, "CR"),
-                     (T.GZ[:, :], 0.0, "GZ"), (T.GV0[:, :], 0.0, "GV0"), (T.GV1[:, :], 0.0, "GV1"), (T.HV0[:, :], 0.0, "HV0"),
-                     (T.NW[:, 0:OFF], 0.0, "NWp0"), (T.NW[:, TOP + 1:W], 0.0, "NWp1")):
-        sfill(ap, x, w)
-    ts(T.NW[:, TOP:TOP + 1], T.MI[:, 12:13], T.MI[:, 14:15], sub, "MI", "NWp2", float(FAR), mult)
-    fill(T.LB[:, :], 0, "GLB JLB")
+    iota(T.F5[:, 0:32], [[1, 4], [4, 8]], 4, 0, "F5", after="UT")
+    iota(T.KB[:, :], [[1, 8], [0, 4], [8, 4]], 0, -1, "KB", after="F5")
+    iota(T.FK[:, :], [[-32, 8], [-8, 5]], 5, 2, "FK", after="KB")
+    iota(T.FB[:, :], [[-48, 8], [-9, 5]], -3, 3, "FB", after="FK")
+    cp(T.L5[:, 0:32], T.F5[:, 0:32], "F5", "L5")
+    LD = T.L5[:, 32:40]
+    ts(LD, T.M2[:, 0:8], 2.5, mult, "M2", "LD", 41.5, add)
+    ts(T.CX[:, 6:7], T.PO[:, 0:1], 3.0, add, "PR0 PO", "CX6", T.PR[:, 0:1], sub)
+    ts(T.CX[:, 7:8], T.CX[:, 6:7], 6.0, eq, "CX6", "CX7")
+    ts(T.CX[:, 0:1], T.CX[:, 6:7], 6.0, op.not_equal, "CX6", "CX0", 0.5, mult)
+    sc(T.F5[:, 32:40], T.M2[:, 0:8], "M2", "F8", bias=70.0, scale=4.0)
+    ts(T.LE[:, :], T.F5[:, 32:40], T.CX[:, 6:7], add, "F8 CX6 CX0", "LE", T.CX[:, 0:1], mult)
+    sfill(T.R5[:, :], -BIG, "R5")
+    sc(T.R5[:, 0::5], T.M2[:, 0:8], "M2", "R5", bias=15.0 / 64 - 0.5, scale=1.0 / 64)
+    for ap, w in ((T.GV0[:, :], "GV0"), (T.GV1[:, :], "GV1"), (T.HV0[:, :], "HV0"), (T.GX[:, 0:1], "GX0"), (T.HX[:, 0:1], "HX0"),
+                  (T.NW[:, 0:OFF], "NWp0"), (T.NW[:, TOP:W], "NWp1"), (T.GTB[:, :], "GTB"), (T.SC[:, :], "SC")):
+        sfill(ap, 0.0, w)
+    fill(T.GLB[:, :], 0, "GLB")
     fill(T.PW[:, 0:OFF], 0, "PWb0")
     fill(T.PW[:, TOP:W], 0, "PWb1")
-    small(T.RK1[:, :], T.FK[:, :], 8, "FK", "RK1")
-    sfill(T.RK1[:, 0::5], 0.0, "RK1")
-    sc(T.RK[:, 0::2], T.RK1[:, :], "RK1", "RKa", scale=-KEY)
-    sc(T.RK[:, 1::2], T.RK1[:, :], "RK1", "RKb", scale=KEY)
+    small(T.RK[:, :], T.FK[:, :], 8, "FK", "RK")
+    sfill(T.RK[:, 0::5], 0.0, "RK")
     small(T.RN1[:, :], T.FB[:, :], 8, "FB", "RN1")
     ts(T.RN2[:, :], T.FB[:, :], 3.0, eq, "FB", "RN2")
     tt(T.RN0[:, :], T.RN1[:, :], T.RN2[:, :], sub, "RN1 RN2", "RN0")
@@ -324,24 +328,27 @@ def rank_program(g, core, T, topo):
     sc(T.GSH[:, :], GS, "GS48", "GSH")
     sc(T.GSF[:, :], GS, "GS48", "GSF")
     sc(T.MIH[0:16, :], T.MI[0:16, :], "MI", "MIH")
+    for f in range(4):
+        sc(T.SC[:, 2 + 4 * f:128:16], GS, "GS48 SC", "SC%d" % f)
 
-    iota(T.CI[:, 0:1], [[0, 1]], 0, 1, "CI0", True)
-    iota(T.IC[:, :], [[1, 128]], 0, 0, "IC", True)
-    for k, ops in enumerate(((15, an), (4, rs), (7, an), (1, an), (1, rs, 7, an))):
-        ts(T.CI[:, k + 1:k + 2], T.CI[:, 0:1], ops[0], ops[1], "CI0", "CI%d" % (k + 1), *ops[2:])
-    cp(T.CF[:, 0:6], T.CI[:, 0:6], "CI0 CI1 CI2 CI3 CI4 CI5", "CF")
-    p15, pg, p7, p1, ph = [T.CF[:, k:k + 1] for k in range(1, 6)]
-    ts(T.CX[:, 1:2], p15, 8.0, mult, "CF", "CX1", pg, add)
-    ts(T.CX[:, 2:3], p1, 8.0, mult, "CF", "CX2", pg, add)
-    ts(T.CX[:, 4:5], T.CX[:, 2:3], 2.0, mult, "CX2", "CX4", -15.0, add)
-    ts(T.CX[:, 3:4], p7, 5.0, mult, "CF", "CX3", -22.0, add)
-    ts(T.IDP[:, :], T.IC[:, :], T.CX[:, 1:2], eq, "IC CX1", "IDP")
-    sc(T.IDQ[:, :], T.IDP[:, :], "IDP", "IDQ")
-    ts(T.MIP[:, :], T.M2[:, :], T.CX[:, 4:5], eq, "M2 CX4", "MIP")
-    ts(T.GSP[:, :], T.IC[:, 0:8], ph, eq, "IC CF", "GSP")
-    ts(T.LP[:, :], T.C26[:, :], T.CX[:, 3:4], add, "C26 CX3", "LP")
-    ts(T.IC3[:, :], T.IC[:, :], 3, rs, "IC", "IC3")
-    ts(T.MI8[:, :], T.IC3[:, :], p15, eq, "IC3 CF", "MI8")
+    def closing():
+        iota(T.CI[:, 0:1], [[0, 1]], 0, 1, "CI0", True, "net")
+        iota(T.IC[:, :], [[1, 128]], 0, 0, "IC", True, "net")
+        for k, ops in enumerate(((15, an), (4, rs), (7, an), (1, an), (1, rs, 7, an))):
+            ts(T.CI[:, k + 1:k + 2], T.CI[:, 0:1], ops[0], ops[1], "CI0", "CI%d" % (k + 1), *ops[2:])
+        cp(T.CF[:, 0:6], T.CI[:, 0:6], "CI0 CI1 CI2 CI3 CI4 CI5", "CF")
+        p15, pg, p7, p1, ph = [T.CF[:, k:k + 1] for k in range(1, 6)]
+        ts(T.CX[:, 1:2], p15, 8.0, mult, "CF", "CX1", pg, add)
+        ts(T.CX[:, 2:3], p1, 8.0, mult, "CF", "CX2", pg, add)
+        ts(T.CX[:, 4:5], T.CX[:, 2:3], 2.0, mult, "CX2", "CX4", -15.0, add)
+        ts(T.CX[:, 3:4], p7, 5.0, mult, "CF", "CX3", -22.0, add)
+        ts(T.IDP[:, :], T.IC[:, :], T.CX[:, 1:2], eq, "IC CX1", "IDP")
+        sc(T.IDQ[:, :], T.IDP[:, :], "IDP", "IDQ")
+        ts(T.MIP[:, :], T.M2[:, :], T.CX[:, 4:5], eq, "M2 CX4", "MIP")
+        ts(T.GSP[:, :], T.IC[:, 0:8], ph, eq, "IC CF", "GSP")
+        ts(T.LP[:, :], T.C26[:, :], T.CX[:, 3:4], add, "C26 CX3", "LP")
+        ts(T.IC3[:, :], T.IC[:, :], 3, rs, "IC", "IC3")
+        ts(T.MI8[:, :], T.IC3[:, :], p15, eq, "IC3 CF", "MI8")
 
     ts(T.NA[0:80, :], T.NT[0:80, :], 10, rs, "NT0 NT1", "NA")
     ts(T.NP[0:80, 64:128], T.NT[0:80, :], 63, an, "NT0 NT1", "NP1")
@@ -354,36 +361,18 @@ def rank_program(g, core, T, topo):
         dma("y", "lnd", T.ND[b:15:3, :], T.NS[0:80, 64 * b:64 * b + 64], "NS%d" % b)
     event("lnd", 3 * 16, "ND", 1.9)
     for b in range(4):
-        bank = "b5" if b % 2 else "b2"
+        bank = "b0" if b % 2 else "b2"
         mm(T[bank][:, 0:256], T.MIH[0:15, :], T.ND[0:15, 256 * b:256 * b + 256], True, True, "MIH ND", bank)
         (cp if b % 2 else sc)(T.NW[:, OFF + 256 * b:OFF + 256 * b + 256], T[bank][:, 0:256], bank, "NW%d" % b)
-    fill(T.PQ[0:96, :], 0, "PQ0")
-    for k in range(8):
-        dma("y", "lpq", T.PQ[0:96:4, 16 * k:16 * k + 16], T.pts[3 * k:3 * k + 3, :], "PQ0", "lnd")
-    event("lpq", 128, "PQ", 1.9)
 
-    sfill(T.PD[96:128, 32 * me:32 * me + 32], 1.0, "PD1", 96)
-    cp(T.PD[0:96, 32 * me:32 * me + 32], T.P4[0:96, :], "P4", "PD0")
-    send(lambda q: mine, lambda q: mine, "pd", "PD0 PD1", "PD", FIRST, "NT1 E48 UT M2 PO")
-    for b in range(4):
-        ts(T.SEL[:, 128 * b:128 * b + 128], T.KD[:, :], float(-b), eq, "KD", "SEL%d" % b)
-    sfill(T.PQH[96:128, :], 1.0, "PQ1", 96)
-    cp(T.PQH[0:96, :], T.PQ[0:96, :], "PQ", "PQH")
-    mm(T.b3[:, 0:128], T.SEL[:, 0:128], T.PQH[:, :], True, True, "SEL0 PQH PQ1", "b3")
-    sc(T.HTB[:, :], T.b3[:, 0:128], "b3", "HTB")
-    for b in range(4):
-        mm(T.b4[:, 32 * b:32 * b + 32], T.SEL[:, 128 * b:128 * b + 128], mine, True, True, "SEL%d PD0 PD1" % b, "b4")
-    sc(T.HTA[:, :], T.b4[:, 0:128], "b4", "HTA")
-    for b in range(4):
-        bank, at = "b%d" % (b // 2), 192 * (b % 2)
-        mm(T[bank][:, at:at + 192], T.SEL[:, 128 * b:128 * b + 128], T.PD[:, :], True, True, "SEL%d PD PD0 PD1" % b, bank)
-        if b % 2:
-            (cp if b // 2 else sc)(T.PTA[:, 192 * b - 192:192 * b + 192], T[bank][:, 0:384], bank, "PTA%d" % (b // 2))
     for k in range(8):
-        sfill(T.QR[:, 128 * k:128 * k + 128], 0.0, "QR%d" % k)
-    for q in others:
-        dma("s", "lqr", T.QR[4 * slot(me, q)::32, :], T.PD[:, 32 * q:32 * q + 32], "PD " + " ".join("QR%d" % k for k in range(8)))
-    event("lqr", 16 * (N - 1), "QR", 1.9)
+        dma("s", "lpq", T.PQ[0:24, 16 * k:16 * k + 16], T.pts[3 * k:3 * k + 3, :], "", "lpl")
+    event("lpq", 128, "PQ", 2 * LOCAL)
+    ts(T.SB[0:32, :], T.KB[0:32, :], 0.0, eq, "KB", "SB")
+    cp(T.PQH[0:24, :], T.PQ[0:24, :], "PQ", "PQH")
+    for bank, src, out in (("b3", "PQH", "HTB"), ("b4", "PH", "HTA")):
+        mm(T[bank][:, 0:128], T.SB[0:24, :], T[src][0:24, :], True, True, "SB " + src, bank)
+        sc(T[out][:, :], T[bank][:, 0:128], bank + " CX7", out, bias=T.CX[:, 7:8], f=act.Identity)
 
     def opened():
         mm(T.b6[:, 0:48], T.ONF[0:1, :], T.CY[0:1, :], True, False, "ONF " + cy, "b6", True)
@@ -397,14 +386,16 @@ def rank_program(g, core, T, topo):
         ms, end = "MS%d" % k, k == R - 1
         small(T.OH[:, :], T.b6[:, 0:48], TT, "b6", "OH")
         mm(T.b7[:, 0:48], T.UT[:, :], T.OH[:, :], True, True, "UT OH", "b7")
-        tt(T.BT[:, 0::2], T.b6[:, 0:48], T.OH[:, :], mult, "b6 OH", "BTt")
-        ts(T.BT[:, 1::2], T.OH[:, :], T.CX[:, 0:1], mult, "CX0 OH", "BTj")
-        scan(T.SS[:, :], T.R6[:, :], T.b7[:, 0:48], mult, hi, "R6 b7", "SS")
-        tt(T.AA[:, 128:256], T.SS[:, :], T.IA[:, :], eq, "SS LA " + ia, "AA", T.LA[:, 0:8])
+        tt(T.BT[:, 0::4], T.b6[:, 0:48], T.OH[:, :], mult, "b6 OH", "BT0")
+        for c in range(3):
+            tt(T.BT[:, 1 + c::4], T.b1[:, 256 + 48 * c:304 + 48 * c], T.OH[:, :], mult, "b1 OH", "BT%d" % (c + 1))
+        scan(T.SS[:, :], T.R6[:, :], T.b7[:, 0:48], 0.0, mult, hi, "R6 b7", "SS")
+        tt(T.AA[:, 128:256], T.SS[:, :], T.IA[:, :], eq, "SS LA IA", "AA", T.LA[:, 0:8])
         for a in range(8):
-            slots(a, T.b7[32 * (a // 2):32 * (a // 2) + 32, 64:76], T.BT[:, 12 * a:12 * a + 12], "BTj BTt", "b7")
-        ts(T[ms][:, :], T.b7[:, 64:76], MID + OFF, add, "b7", ms)
-        send(lambda q: T[ms][:, 2 * q:2 * q + 2], lambda q: T["LM%d" % k][:, 2 * slot(q, me):2 * slot(q, me) + 2], "rq%d" % k, ms + " RL%d0" % k, "LM%d" % k)
+            slots(a, T.b7[32 * (a // 2):32 * (a // 2) + 32, 64:88], T.BT[:, 24 * a:24 * a + 24], "BT0 BT1 BT2 BT3", "b7")
+        cp(T[ms][:, :], T.b7[:, 64:88], "b7", ms)
+        send(lambda q: T[ms][:, 4 * q:4 * q + 4], lambda q: T["LM%d" % k][:, 4 * slot(q, me) + 4:4 * slot(q, me) + 8], "rq%d" % k,
+             ms + " RL%d0" % k, "LM%d" % k, 0.0 if k else FIRST)
         ts(T.HL[:, :], T.b6[:, me:48:6], MID + OFF, add, "b6", "HL", float(TOP), lo)
         sc(T.QI[:, :], T.b6[:, 0:48:6], "b6", "QI", bias=QB, scale=1.0 / TT)
         tt(T.DQ[:, :], T.QI[:, :], T["MIP" if end else "MI"][:, :], mult, "QI LT MI MIP" if end else "QI LT MI", "DQ", T.LT[:, 0:8])
@@ -416,24 +407,23 @@ def rank_program(g, core, T, topo):
         sc(T.AT[:, :], T.b5[:, 0:128], "b5", "AT")
 
     def step(h, i, lst, ln, pt, n, m, kept=False, turned=False, z=None):
-        last = i == S - 1
         bk, bn = ("b3", "b4") if h == "H" else ("b0", "b1")
         X = lambda a: T[h + a]
-        mm(T[bk][0:n, 0:10 * m], T.ON[0:1, 0:n], T.CR[0:1, 0:10 * m], True, False, "ON CR", bk)
+        e = 5 * m
         if kept:
-            mm(T[bn][0:n, 0:5 * m], T.IDF[0:n, 0:n], X("V0")[0:n, 0:5 * m], True, False, "IDF " + h + "V0", bn, True)
-        sc(X("N")[:, 0:n], T.NW[:, :], "NWp0 NWp1 NWp2 NW0 NW1 NW2 NW3 " + ln, h + "N", by=lst)
+            mm(T[bn][0:n, 0:e], T.IDF[0:n, 0:n], X("V0")[0:n, 0:e], True, False, "IDF " + h + "V0", bn, True)
+        sc(X("N")[:, 0:n], T.NW[:, :], "NWp0 NWp1 NW0 NW1 NW2 NW3 " + ln, h + "N", by=lst)
         tt(X("P")[:, 0:n], T.PW[:, :], T[pt][:, 0:n], mult, "PWa PWb0 PWb1 " + ln + " " + pt, h + "P", lst)
-        mm(T[bk][0:n, 0:10 * m], X("P")[0:16 * m, 0:n], T.RK[0:16 * m, 0:10 * m], False, True, h + "P RKa RKb", bk, True)
-        rn = "RNB" if last else "RNA"
-        mm(T[bn][0:n, 0:5 * m], X("N")[0:16 * m, 0:n], T[rn][0:16 * m, 0:5 * m], not kept, not turned, h + "N " + rn, bn)
+        mm(T[bk][0:n, 0:e], X("P")[0:16 * m, 0:n], T.RK[0:16 * m, 0:e], True, True, h + "P RK", bk, True)
+        rn = "RNB" if i == S - 1 else "RNA"
+        mm(T[bn][0:n, 0:e], X("N")[0:16 * m, 0:n], T[rn][0:16 * m, 0:e], not kept, not turned, h + "N " + rn, bn)
         if turned:
             mm(T[bn][0:n, 0:25:5], T.GDF[0:80, :], T.GS48[0:80, 0:30:6], False, True, "GDF GS48", bn, True)
-        scan(X("SC")[0:n, 0:10 * m], T.R5[0:n, 0:10 * m], T[bk][0:n, 0:10 * m], lo, add, "R5 " + bk, h + "SC")
-        ts(X("X")[0:n, 0:5 * m], X("SC")[0:n, 0:10 * m:2], 0.0, op.is_lt, h + "SC", h + "X")
+        scan(X("S")[0:n, 0:e], T.R5[0:n, 0:e], T[bk][0:n, 0:e], -1.0, hi, lo, "R5 " + bk, h + "S")
+        tt(X("X")[0:n, 1:e], X("S")[0:n, 1:e], X("S")[0:n, 0:e - 1], eq, h + "S", h + "X")
         z = z or h + "Z"
-        scan(T[z][0:n, 0:5 * m], X("X")[0:n, 0:5 * m], T[bn][0:n, 0:5 * m], mult, add, h + "X " + bn, z)
-        return T[z][0:n, 4:5 * m:5]
+        scan(T[z][0:n, 0:e], X("X")[0:n, 0:e], T[bn][0:n, 0:e], 0.0, mult, add, h + "X " + h + "X0 " + bn, z)
+        return T[z][0:n, 4:e:5]
 
     def left(out, z, r, w):
         sc(out, z, r, w, bias=float(-FAR), f=act.Relu)
@@ -455,7 +445,7 @@ def rank_program(g, core, T, topo):
             mm(T.b6[0:8, 0:128], T.HV1[:, 0::6], T.IDP[:, :], True, False, "IDP HV10", "b6", True)
         step("H", 2, hl, "HL", "HTB", 128, 8, kept=True)
         if k < R - 1:
-            tt(T.DX[:, :], T.HZ[:, :], T.MI[:, :], mult, "HZ LD MI", "DX", T.LD[:, 0:8])
+            tt(T.DX[:, :], T.HZ[:, :], T.MI[:, :], mult, "HZ LD MI", "DX", LD)
             mm(T.b6[:, 0:48], T.DX[:, :], T.GS48[:, :], False, False, "DX GS48", "b6", True)
         else:
             tt(T.DX[:, :], T.HZ[:, :], T.MI8[:, :], mult, "HZ LP MI8", "DX", T.LP[:, 0:8])
@@ -463,24 +453,25 @@ def rank_program(g, core, T, topo):
 
     def guests(k):
         lm, rt = "LM%d" % k, "RT%d" % k
-        ja, ga = T.JLA[:, 0:5], T.GLA[:, 0:5]
-        cp(ja, T[lm][:, 1::2], lm, "JLA")
-        sc(T.GTA[:, :], T.PTA[:, :], "PTA0 PTA1 JLA", "GTA", by=ja)
-        cp(ga, T[lm][:, 0::2], lm, "GLA")
-        sc(T.GI[:, :], T.IW[:, :], "IW JLA", "GI", by=ja)
-        mm(T.b2[0:80, 0:8], T.GI[:, :], T.IDH[:, 0::16], True, True, "GI IDH", "b2")
-        cp(T.LB[0:80, 8:16], T.b2[0:80, 0:8], "b2", "JLB")
-        sc(T.GTB[:, :], T.PTB[:, :], "PTB0 PTB1 PTB2 PTB3 JLB", "GTB", by=T.LB[:, 8:16])
-        z = step("G", 0, ga, "GLA", "GTA", 80, 8)
-        tt(T.GD[:, :], T.GZ[:, :], T.MI[:, :], mult, "GZ LD MI", "GD", T.LD[:, 0:8])
-        left(T.GV0[0:80, 0::5], z, "GZ", "GV0")
-        mm(T.b2[:, 0:5], T.GD[0:80, :], T.GSF[0:80, 0:5], True, True, "GD GSF", "b2")
-        ts(ga, T.b2[:, 0:5], float(TOP), lo, "b2", "GLA")
-        z = step("G", 1, ga, "GLA", "GTA", 80, 8, kept=True)
-        ts(T.LB[0:80, 0:8], z, float(TOP), lo, "GZ", "GLB")
+        win, ga, gb = T[lm][:, :], T.GLA[:, 0:5], T.GLB[:, 0:8]
+        sc(T.GE[:, :], win, lm + " %s0 LE" % lm, "GE", by=T.LE[:, 0:5])
+        mm(T.b7[0:80, 0:128], T.GE[:, :], T.IDH[:, :], True, True, "GE IDH", "b7")
+        sc(T.GTB[0:80, :], T.b7[0:80, 0:128], "b7", "GTB")
+        tt(T.GD[:, :], win, T.MI[:, 0:80], mult, lm + " %s0 L5 MI" % lm, "GD", T.L5[:, 0:5])
+        mm(T.b2[0:80, 0:8], T.GD[:, :], T.GSF[:, :], True, True, "GD GSF", "b2")
+        ts(T.GLB[0:80, :], T.b2[0:80, 0:8], MID + OFF, add, "b2", "GLB")
+        for c in range(3):
+            tt(T.GY[:, 80 * c:80 * c + 80], win, T.MI[:, 0:80], mult, lm + " %s0 L5 MI" % lm, "GY%d" % c, T.L5[:, 8 * c + 8:8 * c + 13])
+            mm(T.b2[:, 0:80], T.SC[:, 2 - c:130 - c], T.GY[:, 80 * c:80 * c + 80], c == 0, c == 2, "SC SC0 SC1 SC2 SC3 GY%d" % c, "b2")
+        sc(T.GTA[:, :], T.b2[:, 0:80], "b2 CX7", "GTA", bias=T.CX[:, 7:8], f=act.Identity)
+        z = step("G", 0, gb, "GLB", "GTB", 128, 5)
+        ts(ga, z, float(TOP), lo, "GZ", "GLA")
+        left(T.GV0[:, 0:25:5], z, "GZ", "GV0")
+        z = step("G", 1, ga, "GLA", "GTA", 80, 8)
+        ts(T.GLB[0:80, :], z, float(TOP), lo, "GZ", "GLB")
         left(T.GV1[0:80, :], z, "GZ", "GV1")
         tt(T.GDF[:, :], T.GV1[:, :], T.MI[:, :], mult, "GV1 LT MI", "GDF", T.LT[:, 0:8])
-        step("G", 2, T.LB[:, 0:8], "GLB", "GTB", 128, 5, turned=True, z=rt)
+        step("G", 2, gb, "GLB", "GTB", 128, 5, kept=True, turned=True, z=rt)
         send(lambda q: T[rt][:, 5 * slot(me, q) + 4:5 * slot(me, q) + 5], lambda q: T["RL%d" % k][:, me:me + 1], "rt%d" % k, rt, "RL%d" % k)
 
     def replies(k):
@@ -495,13 +486,9 @@ def rank_program(g, core, T, topo):
     mm(T.b6[:, 0:48], T.DX[:, :], T.GS48[:, :], False, True, "DX GS48", "b6", True)
     for k in range(R):
         dispatch(k)
-        if k == 0:
-            iota(T.IW[:, :], [[32, 4], [0, 6], [1, 32]], 0, 8, "IW", after="net FB")
-            for b in range(4):
-                bank = T["b7" if b % 2 else "b6"][:, 0:256]
-                mm(bank, T.SEL[:, 0:128], T.QR[:, 256 * b:256 * b + 256], True, True, "SEL0 QR", "b7" if b % 2 else "b6")
-                sc(T.PTB[:, 256 * b:256 * b + 256], bank, "b7" if b % 2 else "b6", "PTB%d" % b)
         guests(k)
+        if k == 0:
+            closing()
         home(k)
         replies(k)
     cp(T.YS[0:8, :], T.b6[0:8, 0:128], "b6", "YS")

@@ -10,7 +10,7 @@ BIG = 2.0 ** 30
 MID = 511.5
 QB = 129.0
 CYC = 1.04e-3
-LAT, LOCAL, HOP, ISSUE, FIRST = 0.11, 1.6, 1.9, 0.5, 1.0
+LAT, LOCAL, HOP, ISSUE, FIRST = 0.2, 1.6, 1.8, 0.5, 1.0
 
 
 def _s(n, dtype="float32"):
@@ -38,10 +38,12 @@ SCRATCH = {
 for _t in "HG":
     SCRATCH.update({_t + "P": _s(128), _t + "N": _s(128, "bfloat16"), _t + "S": _s(40), _t + "X": _s(40), _t + "Z": _s(40), _t + "V0": _s(40)})
 for _k in range(R):
-    SCRATCH["MS%d" % _k] = _s(24)
-    SCRATCH["LM%d" % _k] = _s(24)
+    SCRATCH["LH%d" % _k] = _s(60, "float16")
+    SCRATCH["MS%d" % _k] = _s(24, "float16")
+    SCRATCH["RC%d" % _k] = _s(8)
+    SCRATCH["LM%d" % _k] = _s(64)
     SCRATCH["RT%d" % _k] = _s(25)
-    SCRATCH["RL%d" % _k] = _s(8)
+    SCRATCH["RL%d" % _k] = _s(32)
 for _k in range(8):
     SCRATCH["b%d" % _k] = ("psum", [128, 512], "float32")
 
@@ -50,8 +52,9 @@ SEMAPHORES = (["v", "t", "s", "c", "ltet", "lpts", "lpq", "lpl", "lnt", "lnd", "
 BANKS = ["b%d" % k for k in range(8)]
 
 
-def slot(owner, other):
-    return other - (1 if other > owner else 0)
+def sides(topo, cores, owner):
+    far = [q for q in range(N) if topo.chip(cores[q]) != topo.chip(cores[owner])]
+    return far, [q for q in range(N) if q not in far and q != owner]
 
 
 def coarse(u):
@@ -232,12 +235,28 @@ def rank_program(g, core, T, topo):
     split = engine_split(topo, core, [cores[q] for q in others])
     into = sum(len(engine_split(topo, cores[q], [c for c in cores if c != cores[q]])[core]) for q in others)
     sent = [0]
+    slot = lambda owner, other: sum(sides(topo, cores, owner), []).index(other)
+    far, near = sides(topo, cores, me)
+    out_engines = topo.engines(core, cores[far[0]])
+    masks = (out_engines, [e for e in topo.engines(core, cores[near[0]]) if e not in out_engines])
+
+    def spread(src, dst, sem, r, w, first=0.0):
+        def go():
+            need("c", r.split(), [])
+            tr = []
+            for i, ranks in enumerate((far, near)):
+                tr.append(RemoteDMATransfer(dst_ids=[DstId(rid=topo.addr(cores[q])[0], pnc=topo.addr(cores[q])[1]) for q in ranks],
+                                            dma_engine_mask=sum(1 << e for e in masks[i]), remote_sem=T.sem[sem], srcs=[src(i)], dsts=[dst(q) for q in ranks]))
+                sent[0] += len(masks[i])
+            g.remote_dma_fused(tr, local_sem=T.sem.sent)
+        dmas[sem] = [note("c", ISSUE + first, 0.0, r.split(), ["net"], go)]
+        event(sem, len(far) * len(masks[0]) + len(near) * len(masks[1]), w, HOP)
 
     def send(src, dst, sem, r, w, first=0.0):
         def go():
             need("c", r.split(), [])
             tr = []
-            for q in others:
+            for q in sorted(others, key=lambda q: topo.chip(cores[q]) == topo.chip(core)):
                 rid, pid = topo.addr(cores[q])[:2]
                 tr.append(RemoteDMATransfer(dst_ids=[DstId(rid=rid, pnc=pid)], dma_engine_mask=sum(1 << e for e in split[cores[q]]),
                                             remote_sem=T.sem[sem], src=src(q), dst=dst(q)))
@@ -254,11 +273,13 @@ def rank_program(g, core, T, topo):
         dma("y" if c % 2 else "s", "lpts", T.P3[8 * c:8 * c + 8, :], T.pts[c::3, :])
     dma("y", "lnt", T.NT[16:80, :], T.nbr[:, :])
     for k in range(8):
+        dma("s", "lpq", T.PQ[0:24, 16 * k:16 * k + 16], T.pts[3 * k:3 * k + 3, :], "", "ltet lnt lpts")
+    event("lpq", 128, "PQ", 2.2)
+    for k in range(4):
         dma("y", "lpl", T.PW[16 * k:16 * k + 16, OFF:TOP], T.planes[:, :], "", "ltet lnt lpts")
     event("lpts", 48, "P3", 1.8)
     event("ltet", 16, "T0I")
     event("lnt", 16, "NT0", 1.9)
-    event("lpl", 128, "PWa", 2 * LOCAL)
 
     fill(T.ON[:, :], 1.0, "ON")
     iota(T.PO[:, :], [[-4, 4]], -3, 2, "PO")
@@ -290,12 +311,13 @@ def rank_program(g, core, T, topo):
     sfill(T.AA[:, 256:384], 0.0, "AA1")
     for k in range(R):
         sfill(T["RL%d" % k][:, :], 0.0, "RL%d0" % k)
+        sfill(T["RC%d" % k][:, 5:6], 0.0, "RC%d0" % k)
         sfill(T["LM%d" % k][:, 0:4], 1.0, "LM%d0" % k)
     ts(T.SX[0:32, :], T.KX[0:32, :], 0.0, eq, "KX", "SX")
     cp(T.PH[0:24, :], T.P3[0:24, :], "P3", "PH")
     mm(T.b1[:, 256:400], T.PH[0:24, :], T.SX[0:24, :], True, True, "PH SX", "b1")
 
-    iota(T.F5[:, 0:32], [[1, 4], [4, 8]], 4, 0, "F5", after="UT")
+    iota(T.F5[:, 0:32], [[1, 4], [12, 8]], 4 + 4 * (me - min(near + [me])), 0, "F5", after="UT")
     iota(T.KB[:, :], [[1, 8], [0, 4], [8, 4]], 0, -1, "KB", after="F5")
     iota(T.FK[:, :], [[-32, 8], [-8, 5]], 5, 2, "FK", after="KB")
     iota(T.FB[:, :], [[-48, 8], [-9, 5]], -3, 3, "FB", after="FK")
@@ -305,7 +327,7 @@ def rank_program(g, core, T, topo):
     ts(T.CX[:, 6:7], T.PO[:, 0:1], 3.0, add, "PR0 PO", "CX6", T.PR[:, 0:1], sub)
     ts(T.CX[:, 7:8], T.CX[:, 6:7], 6.0, eq, "CX6", "CX7")
     ts(T.CX[:, 0:1], T.CX[:, 6:7], 6.0, op.not_equal, "CX6", "CX0", 0.5, mult)
-    sc(T.F5[:, 32:40], T.M2[:, 0:8], "M2", "F8", bias=70.0, scale=4.0)
+    sc(T.F5[:, 32:40], T.M2[:, 0:8], "M2", "F8", bias=190.0 + 8 * (me - min(near + [me])), scale=12.0)
     ts(T.LE[:, :], T.F5[:, 32:40], T.CX[:, 6:7], add, "F8 CX6 CX0", "LE", T.CX[:, 0:1], mult)
     sfill(T.R5[:, :], -BIG, "R5")
     sc(T.R5[:, 0::5], T.M2[:, 0:8], "M2", "R5", bias=15.0 / 64 - 0.5, scale=1.0 / 64)
@@ -360,14 +382,14 @@ def rank_program(g, core, T, topo):
     for b in (1, 2, 0):
         dma("y", "lnd", T.ND[b:15:3, :], T.NS[0:80, 64 * b:64 * b + 64], "NS%d" % b)
     event("lnd", 3 * 16, "ND", 1.9)
+    for k in range(4, 8):
+        dma("y", "lpl", T.PW[16 * k:16 * k + 16, OFF:TOP], T.planes[:, :], "", "lnd")
+    event("lpl", 128, "PWa", 2 * LOCAL)
     for b in range(4):
         bank = "b0" if b % 2 else "b2"
         mm(T[bank][:, 0:256], T.MIH[0:15, :], T.ND[0:15, 256 * b:256 * b + 256], True, True, "MIH ND", bank)
         (cp if b % 2 else sc)(T.NW[:, OFF + 256 * b:OFF + 256 * b + 256], T[bank][:, 0:256], bank, "NW%d" % b)
 
-    for k in range(8):
-        dma("s", "lpq", T.PQ[0:24, 16 * k:16 * k + 16], T.pts[3 * k:3 * k + 3, :], "", "lpl")
-    event("lpq", 128, "PQ", 2 * LOCAL)
     ts(T.SB[0:32, :], T.KB[0:32, :], 0.0, eq, "KB", "SB")
     cp(T.PQH[0:24, :], T.PQ[0:24, :], "PQ", "PQH")
     for bank, src, out in (("b3", "PQH", "HTB"), ("b4", "PH", "HTA")):
@@ -394,13 +416,15 @@ def rank_program(g, core, T, topo):
         for a in range(8):
             slots(a, T.b7[32 * (a // 2):32 * (a // 2) + 32, 64:88], T.BT[:, 24 * a:24 * a + 24], "BT0 BT1 BT2 BT3", "b7")
         cp(T[ms][:, :], T.b7[:, 64:88], "b7", ms)
-        send(lambda q: T[ms][:, 4 * q:4 * q + 4], lambda q: T["LM%d" % k][:, 4 * slot(q, me) + 4:4 * slot(q, me) + 8], "rq%d" % k,
-             ms + " RL%d0" % k, "LM%d" % k, 0.0 if k else FIRST)
+        block = lambda i: 4 * min((far, near + [me])[i])
+        spread(lambda i: T[ms][:, block(i):block(i) + 12], lambda q: T["LH%d" % k][:, 12 * slot(q, me):12 * slot(q, me) + 12], "rq%d" % k,
+               ms + " RL%d0" % k, "LH%d" % k, 0.0 if k else FIRST)
+        cp(T["LM%d" % k][:, 4:64], T["LH%d" % k][:, :], "LH%d" % k, "LM%d" % k)
         ts(T.HL[:, :], T.b6[:, me:48:6], MID + OFF, add, "b6", "HL", float(TOP), lo)
-        sc(T.QI[:, :], T.b6[:, 0:48:6], "b6", "QI", bias=QB, scale=1.0 / TT)
+        sc(T.QI[:, :], T.b6[:, 0:48:6], "b6 BT0 HL", "QI", bias=QB, scale=1.0 / TT)
         tt(T.DQ[:, :], T.QI[:, :], T["MIP" if end else "MI"][:, :], mult, "QI LT MI MIP" if end else "QI LT MI", "DQ", T.LT[:, 0:8])
         mm(T.b5[:, 0:8], T.DQ[:, :], T["GSP" if end else "GSH"][:, :], True, True, "DQ GSH GSP" if end else "DQ GSH", "b5")
-        ts(T.LI[:, :], T.b5[:, 0:8], -QB, add, "b5", "LI")
+        ts(T.LI[:, :], T.b5[:, 0:8], 5.0, mult, "b5", "LI", 2 - 5 * QB, add)
         ident = "IDQ" if end else "IDH"
         for a in range(8):
             slots(a, T.b5[32 * (a // 2):32 * (a // 2) + 32, 0:128], T[ident][:, :], ident, "b5")
@@ -455,24 +479,27 @@ def rank_program(g, core, T, topo):
         lm, rt = "LM%d" % k, "RT%d" % k
         win, ga, gb = T[lm][:, :], T.GLA[:, 0:5], T.GLB[:, 0:8]
         sc(T.GE[:, :], win, lm + " %s0 LE" % lm, "GE", by=T.LE[:, 0:5])
-        mm(T.b7[0:80, 0:128], T.GE[:, :], T.IDH[:, :], True, True, "GE IDH", "b7")
-        sc(T.GTB[0:80, :], T.b7[0:80, 0:128], "b7", "GTB")
         tt(T.GD[:, :], win, T.MI[:, 0:80], mult, lm + " %s0 L5 MI" % lm, "GD", T.L5[:, 0:5])
         mm(T.b2[0:80, 0:8], T.GD[:, :], T.GSF[:, :], True, True, "GD GSF", "b2")
+        for a, bank, copy in ((0, "b7", sc), (64, "b0", cp)):
+            mm(T[bank][0:80, 0:64], T.GE[:, :], T.IDH[:, a:a + 64], True, True, "GE IDH", bank)
+            copy(T.GTB[0:80, a:a + 64], T[bank][0:80, 0:64], bank + " GTB", "GTB%d" % a)
         ts(T.GLB[0:80, :], T.b2[0:80, 0:8], MID + OFF, add, "b2", "GLB")
         for c in range(3):
             tt(T.GY[:, 80 * c:80 * c + 80], win, T.MI[:, 0:80], mult, lm + " %s0 L5 MI" % lm, "GY%d" % c, T.L5[:, 8 * c + 8:8 * c + 13])
             mm(T.b2[:, 0:80], T.SC[:, 2 - c:130 - c], T.GY[:, 80 * c:80 * c + 80], c == 0, c == 2, "SC SC0 SC1 SC2 SC3 GY%d" % c, "b2")
         sc(T.GTA[:, :], T.b2[:, 0:80], "b2 CX7", "GTA", bias=T.CX[:, 7:8], f=act.Identity)
-        z = step("G", 0, gb, "GLB", "GTB", 128, 5)
+        z = step("G", 0, gb, "GLB GTB0 GTB64", "GTB", 128, 5)
         ts(ga, z, float(TOP), lo, "GZ", "GLA")
         left(T.GV0[:, 0:25:5], z, "GZ", "GV0")
         z = step("G", 1, ga, "GLA", "GTA", 80, 8)
         ts(T.GLB[0:80, :], z, float(TOP), lo, "GZ", "GLB")
         left(T.GV1[0:80, :], z, "GZ", "GV1")
         tt(T.GDF[:, :], T.GV1[:, :], T.MI[:, :], mult, "GV1 LT MI", "GDF", T.LT[:, 0:8])
-        step("G", 2, gb, "GLB", "GTB", 128, 5, kept=True, turned=True, z=rt)
-        send(lambda q: T[rt][:, 5 * slot(me, q) + 4:5 * slot(me, q) + 5], lambda q: T["RL%d" % k][:, me:me + 1], "rt%d" % k, rt, "RL%d" % k)
+        step("G", 2, gb, "GLB GTB0 GTB64", "GTB", 128, 5, kept=True, turned=True, z=rt)
+        cp(T["RC%d" % k][:, 0:5], T[rt][:, 4::5], rt, "RC%d" % k)
+        at = lambda q: 5 * me + 2 - slot(me, q) % 3
+        spread(lambda i: T["RC%d" % k][:, 3 * i:3 * i + 3], lambda q: T["RL%d" % k][:, at(q):at(q) + 3], "rt%d" % k, "RC%d RC%d0" % (k, k), "RL%d" % k)
 
     def replies(k):
         tt(T.XR[:, :], T["RL%d" % k][:, :], T.AT[:, :], mult, "RL%d RL%d0 LI AT" % (k, k), "XR", T.LI[:, 0:8])

from concourse.bass import DstId, RemoteDMATransfer
from concourse.mybir import AluOpType, ActivationFunctionType

N, TT, P, R, S = 6, 1024, 128, 3, 3
OFF = 64
TOP = TT + OFF
W = TOP + 8
FAR = 2048
BIG = 2.0 ** 30
MID = 511.5
QB = 129.0
CYC = 1.04e-3
LAT, LOCAL, HOP, ISSUE, FIRST = 0.2, 1.6, 1.8, 0.5, 1.0


def _s(n, dtype="float32"):
    return ("sbuf", [128, n], dtype)


SCRATCH = {
    "PW": _s(W, "int32"), "NW": _s(W, "bfloat16"), "T0I": _s(8, "int32"),
    "NT": _s(64, "int32"), "NA": _s(64, "int32"), "NU": _s(64), "NP": _s(128, "int32"), "NS": _s(192, "bfloat16"),
    "ND": _s(TT, "bfloat16"), "MIH": _s(128, "bfloat16"),
    "P3": _s(128, "int32"), "PH": _s(128, "float16"), "PQ": _s(128, "int32"), "PQH": _s(128, "float16"), "HTA": _s(128), "HTB": _s(128),
    "PO": _s(4), "PR": _s(4), "CX": _s(8), "DC": _s(128), "M2": _s(128), "E48": _s(48), "FK": _s(40), "FB": _s(40), "F5": _s(40), "C26": _s(8),
    "KX": _s(144), "KB": _s(128), "SX": _s(144, "float16"), "SB": _s(128, "float16"), "SC": _s(132, "float16"),
    "CI": _s(10, "int32"), "CF": _s(10), "IC": _s(128, "int32"), "IC3": _s(128, "int32"),
    "MI": _s(128), "MIP": _s(128), "MI8": _s(128), "IA": _s(128), "IDF": _s(128), "IDH": _s(128, "float16"), "IDP": _s(128), "IDQ": _s(128, "float16"),
    "UT": _s(128, "bfloat16"), "GSH": _s(8, "bfloat16"), "GSP": _s(8, "bfloat16"), "GSF": _s(8, "float16"), "GS48": _s(48), "CY": _s(48), "ONF": _s(128),
    "RK": _s(40), "RN0": _s(40), "RN1": _s(40), "RN2": _s(40), "RNA": _s(40, "bfloat16"), "RNB": _s(40, "bfloat16"),
    "ON": _s(132, "bfloat16"), "R5": _s(40), "R6": _s(48),
    "LA": _s(8, "uint16"), "L5": _s(40, "uint16"), "LT": _s(8, "uint16"), "LP": _s(8, "uint16"), "LI": _s(8, "uint16"), "LE": _s(8, "uint16"),
    "HL": _s(8, "uint16"), "GLA": _s(8, "uint16"), "GLB": _s(8, "uint16"),
    "QI": _s(8, "bfloat16"), "OH": _s(48, "bfloat16"), "BT": _s(192, "float16"), "SS": _s(48),
    "AA": _s(384, "float16"), "AT": _s(128), "DX": _s(128), "DQ": _s(128, "bfloat16"), "XR": _s(128), "YS": _s(128),
    "GTA": _s(80), "GTB": _s(128), "GE": _s(80, "float16"), "GY": _s(240, "float16"), "GD": _s(80, "float16"), "GDF": _s(128), "GV1": _s(8), "HV1": _s(48),
}
for _t in "HG":
    SCRATCH.update({_t + "P": _s(128), _t + "N": _s(128, "bfloat16"), _t + "S": _s(40), _t + "X": _s(40), _t + "Z": _s(40), _t + "V0": _s(40)})
for _k in range(R):
    SCRATCH["LH%d" % _k] = _s(60, "float16")
    SCRATCH["MS%d" % _k] = _s(24, "float16")
    SCRATCH["RC%d" % _k] = _s(8)
    SCRATCH["LM%d" % _k] = _s(64)
    SCRATCH["RT%d" % _k] = _s(25)
    SCRATCH["RL%d" % _k] = _s(32)
for _k in range(8):
    SCRATCH["b%d" % _k] = ("psum", [128, 512], "float32")

SEMAPHORES = (["v", "t", "s", "c", "ltet", "lpts", "lpq", "lpl", "lnt", "lnd", "sty", "sent"]
              + ["rq%d" % k for k in range(R)] + ["rt%d" % k for k in range(R)])
BANKS = ["b%d" % k for k in range(8)]


def sides(topo, cores, owner):
    far = [q for q in range(N) if topo.chip(cores[q]) != topo.chip(cores[owner])]
    return far, [q for q in range(N) if q not in far and q != owner]


def coarse(u):
    return 1.5 * 2.0 ** 23 * u


def engine_split(topo, src, dsts):
    on = [d for d in dsts if topo.chip(d) == topo.chip(src)]
    off = [d for d in dsts if topo.chip(d) != topo.chip(src)]
    eo = topo.engines(src, off[0])
    out = {}
    for ds, es in ((off, eo), (on, [e for e in topo.engines(src, on[0]) if e not in eo])):
        per = 1
        while 2 * per * len(ds) <= len(es):
            per *= 2
        for i, d in enumerate(ds):
            out[d] = es[i * per:(i + 1) * per]
    return out


def in_order(calls):
    tail = [0.0] * len(calls)
    for i in range(len(calls) - 1, -1, -1):
        q, cost, delay, before = calls[i]
        tail[i] += cost + delay
        for b in before:
            tail[b] = max(tail[b], tail[i])
    start, busy = {}, {}
    for i in sorted(range(len(calls)), key=lambda i: (-tail[i], i)):
        q, cost, delay, before = calls[i]
        t = max([0.0] + [start[b] + calls[b][1] + (0.0 if q == calls[b][0] in ("t", "c") else calls[b][2]) for b in before])
        for a, e in sorted(busy.get(q, [])):
            if t + cost <= a:
                break
            t = max(t, e)
        start[i] = t
        if q:
            busy.setdefault(q, []).append((t, t + cost))
    return sorted(range(len(calls)), key=lambda i: (start[i], i))


def rank_program(g, core, T, topo):
    me = T.rank_of(core)
    if me is None:
        return
    cores = list(T.cores)
    others = [q for q in range(N) if q != me]
    op = AluOpType
    act = ActivationFunctionType
    rel = float(OFF - TT * me)

    calls, issue, last_w, last_r, dmas = [], [], {}, {}, {}

    def note(q, cost, delay, r, w, fn, more=()):
        before = set(more)
        for k in r + w:
            before.update(last_w.get(k, []))
        for k in w:
            before.update(last_r.get(k, []))
        i = len(calls)
        calls.append((q, cost, delay, sorted(before)))
        issue.append(fn)
        for k in r:
            last_r.setdefault(k, []).append(i)
        for k in w:
            last_w[k], last_r[k] = [i], []
        return i

    queues = {"v": g.vector, "t": g.tensor, "s": g.scalar, "c": g, "y": g.sync}
    known = {q: {} for q in queues}
    count = {q: 0 for q in queues}
    clocks, writers, readers = {}, {}, {}

    def wait(q, s, n):
        queues[q].wait_ge(T.sem[s], n)
        for a, b in clocks[(s, n)].items():
            known[q][a] = max(b, known[q].get(a, 0))

    def need(q, r, w):
        ev = []
        for k in r:
            ev += writers.get(k, [])
            if k in BANKS:
                ev += [e for e in readers.get(k, []) if e[0] != q]
        for k in w:
            ev += writers.get(k, [])
            ev += [e for e in readers.get(k, []) if e[0] != q]
        top = {}
        for s, n in ev:
            if not (q == "t" and s == "t"):
                top[s] = max(n, top.get(s, 0))
        for s, n in sorted(top.items(), key=lambda e: e[0]):
            if known[q].get(s, 0) >= n:
                continue
            if any(o != s and known[q].get(o, 0) < m and clocks[(o, m)].get(s, 0) >= n for o, m in top.items()):
                continue
            wait(q, s, n)

    def do(q, fn, r, w, cost, after=""):
        r, w = r.split(), w.split()

        def go():
            need(q, r, w)
            fn(queues[q]).then_inc(T.sem[q], 1)
            count[q] += 1
            ev = (q, count[q])
            clocks[ev] = dict(known[q])
            clocks[ev][q] = count[q]
            for k in r:
                readers.setdefault(k, []).append(ev)
            for k in w:
                writers[k] = [ev]
                readers[k] = []
        note(q, cost, LAT, r, w, go, [i for k in after.split() for i in last_w[k]])

    def event(sem, total, w, delay=LOCAL):
        def go():
            clocks[(sem, total)] = {sem: total}
            for k in w.split():
                writers[k] = [(sem, total)]
                readers[k] = []
        note(None, 0.0, delay, [], w.split(), go, dmas[sem])

    def dma(q, sem, out, in_, r="", after=""):
        def go():
            need(q, r.split(), [])
            queues[q].dma_start(out, in_).then_inc(T.sem[sem], 16)
        dmas.setdefault(sem, []).append(note(q, 0.05, 0.0, r.split(), [], go, [i for s in after.split() for i in dmas[s]]))

    def width(ap):
        return ap.shape[1]

    def plain(n):
        return max(n, 64) * CYC

    def picked(n):
        return 0.06 + 1.56 * n * CYC

    def tt(out, a, b, o, r, w, by=None):
        n = width(out)
        both = 1 if any(k in BANKS for k in r.split()) else 2
        do("v", lambda e: e.tensor_tensor(out=out, in0=a if by is None else a.indirect(by), in1=b, op=o), r, w, plain(both * n) if by is None else picked(n))

    def ts(out, a, s1, o0, r, w, s2=None, o1=None):
        if o1 is None:
            do("v", lambda e: e.tensor_scalar(out, a, s1, None, op0=o0), r, w, plain(width(out)))
        else:
            do("v", lambda e: e.tensor_scalar(out, a, s1, s2, op0=o0, op1=o1), r, w, plain(width(out)))

    def small(out, a, u, r, w):
        ts(out, a, coarse(u), op.add, r, w, coarse(u), op.is_equal)

    def cp(out, a, r, w):
        do("v", lambda e: e.tensor_copy(out, a), r, w, plain(width(out)))

    def fill(ap, x, w):
        do("v", lambda e: e.memset(ap, x), "", w, plain(width(ap)))

    def sc(out, a, r, w, bias=0.0, scale=1.0, f=act.Copy, by=None):
        n = width(out)
        do("s", lambda e: e.activation(out, a if by is None else a.indirect(by), f, bias=bias, scale=scale), r, w, plain(n) if by is None else picked(n))

    def sfill(ap, x, w):
        sc(ap, T.ON[0:ap.shape[0], 0:width(ap)], "ON", w, bias=float(x), scale=0.0)

    def scan(out, d0, d1, first, o0, o1, r, w):
        do("v", lambda e: e.tensor_tensor_scan(out, d0, d1, first, o0, o1), r, w, plain(width(out)))

    def mm(out, lhsT, rhs, start, stop, r, w, wide=False):
        do("t", lambda e: e.matmul(out, lhsT, rhs, start, stop), r, w, max(min(64, out.shape[0]), width(out)) * (4 if wide else 1) * CYC)

    def iota(out, pattern, base, cm, w, whole=False, after=""):
        if whole:
            do("c", lambda e: e.iota(out, pattern, base, cm), "", w, 0.13 + 2 * width(out) * CYC, after)
        else:
            do("c", lambda e: e.iota(out, pattern, base, cm, allow_small_or_imprecise_dtypes=True), "", w, 0.13 + 2 * width(out) * CYC, after)

    split = engine_split(topo, core, [cores[q] for q in others])
    into = sum(len(engine_split(topo, cores[q], [c for c in cores if c != cores[q]])[core]) for q in others)
    sent = [0]
    slot = lambda owner, other: sum(sides(topo, cores, owner), []).index(other)
    far, near = sides(topo, cores, me)
    out_engines = topo.engines(core, cores[far[0]])
    masks = (out_engines, [e for e in topo.engines(core, cores[near[0]]) if e not in out_engines])

    def spread(src, dst, sem, r, w, first=0.0):
        def go():
            need("c", r.split(), [])
            tr = []
            for i, ranks in enumerate((far, near)):
                tr.append(RemoteDMATransfer(dst_ids=[DstId(rid=topo.addr(cores[q])[0], pnc=topo.addr(cores[q])[1]) for q in ranks],
                                            dma_engine_mask=sum(1 << e for e in masks[i]), remote_sem=T.sem[sem], srcs=[src(i)], dsts=[dst(q) for q in ranks]))
                sent[0] += len(masks[i])
            g.remote_dma_fused(tr, local_sem=T.sem.sent)
        dmas[sem] = [note("c", ISSUE + first, 0.0, r.split(), ["net"], go)]
        event(sem, len(far) * len(masks[0]) + len(near) * len(masks[1]), w, HOP)

    def send(src, dst, sem, r, w, first=0.0):
        def go():
            need("c", r.split(), [])
            tr = []
            for q in sorted(others, key=lambda q: topo.chip(cores[q]) == topo.chip(core)):
                rid, pid = topo.addr(cores[q])[:2]
                tr.append(RemoteDMATransfer(dst_ids=[DstId(rid=rid, pnc=pid)], dma_engine_mask=sum(1 << e for e in split[cores[q]]),
                                            remote_sem=T.sem[sem], src=src(q), dst=dst(q)))
                sent[0] += len(split[cores[q]])
            g.remote_dma_fused(tr, local_sem=T.sem.sent)
        dmas[sem] = [note("c", ISSUE + first, 0.0, r.split(), ["net"], go)]
        event(sem, into, w, HOP)

    rs, an = op.arith_shift_right, op.bitwise_and
    add, sub, mult, eq, lo, hi = op.add, op.subtract, op.mult, op.is_equal, op.min, op.max

    dma("y", "ltet", T.T0I[:, :], T.tet0[:, :])
    for c in range(3):
        dma("y" if c % 2 else "s", "lpts", T.P3[8 * c:8 * c + 8, :], T.pts[c::3, :])
    dma("y", "lnt", T.NT[16:80, :], T.nbr[:, :])
    for k in range(8):
        dma("s", "lpq", T.PQ[0:24, 16 * k:16 * k + 16], T.pts[3 * k:3 * k + 3, :], "", "ltet lnt lpts")
    event("lpq", 128, "PQ", 2.2)
    for k in range(4):
        dma("y", "lpl", T.PW[16 * k:16 * k + 16, OFF:TOP], T.planes[:, :], "", "ltet lnt lpts")
    event("lpts", 48, "P3", 1.8)
    event("ltet", 16, "T0I")
    event("lnt", 16, "NT0", 1.9)

    fill(T.ON[:, :], 1.0, "ON")
    iota(T.PO[:, :], [[-4, 4]], -3, 2, "PO")
    iota(T.M2[:, :], [[0, 8], [2, 16]], -15, 0, "M2", after="PO")
    iota(T.E48[:, :], [[-32, 8], [0, 6]], -15, 2, "E48", after="M2")
    iota(T.DC[:, :], [[1, 128]], 0, -1, "DC", after="E48")
    iota(T.NT[0:16, :], [[1, 64]], TT * me, 64, "NT1", True, after="DC")
    iota(T.KX[:, :], [[8, 3], [1, 8], [0, 6]], 0, -1, "KX", after="NT1")
    for k, u in ((0, 8), (1, 16), (3, 32)):
        ts(T.PR[:, k:k + 1], T.PO[:, k:k + 1], coarse(u), add, "PO", "PR%d" % k, coarse(u), sub)
    ts(T.LT[:, :], T.M2[:, 0:8], 0.5, mult, "M2", "LT", 7.5, add)
    ts(T.MI[:, :], T.M2[:, :], T.PR[:, 3:4], add, "M2 PR3 PO", "MI", T.PO[:, 3:4], eq)
    small(T.GS48[:, :], T.E48[:, :], 32, "E48", "GS48")
    GS = T.GS48[:, 0::6]
    sfill(T.ONF[0:1, :], 1.0, "ONF")
    for q in range(N):
        fill(T.CY[0:1, q::6], -TT * q - MID, "CY%d" % q)
    cy = " ".join("CY%d" % q for q in range(N))
    ts(T.UT[:, :], T.DC[:, :], 0.0, eq, "DC", "UT", 4096.0, mult)
    do("c", lambda e: e.affine_select(T.UT[:, :], T.UT[:, :], [[-1, 128]], op.is_ge, 16.0, 0, 1), "UT", "UT", 0.17 + 256 * CYC, "KX")
    sfill(T.R6[:, :], 1.0, "R6")
    sfill(T.R6[:, 0::6], 0.0, "R6")
    sfill(T.C26[:, :], 26.0, "C26")
    ts(T.CX[:, 5:6], T.PR[:, 1:2], T.PO[:, 1:2], sub, "PR1 PO", "CX5", -3.0, mult)
    ts(T.LA[:, :], T.C26[:, :], T.CX[:, 5:6], add, "C26 CX5", "LA")
    ts(T.IA[:, :], T.DC[:, :], 2.0, mult, "DC PO", "IA", T.PO[:, 1:2], add)
    ts(T.IA[:, :], T.IA[:, :], coarse(16), add, "IA", "IA", coarse(16) - 4096, sub)
    sfill(T.AA[:, 0:128], 0.0, "AA0")
    sfill(T.AA[:, 256:384], 0.0, "AA1")
    for k in range(R):
        sfill(T["RL%d" % k][:, :], 0.0, "RL%d0" % k)
        sfill(T["RC%d" % k][:, 5:6], 0.0, "RC%d0" % k)
        sfill(T["LM%d" % k][:, 0:4], 1.0, "LM%d0" % k)
    ts(T.SX[0:32, :], T.KX[0:32, :], 0.0, eq, "KX", "SX")
    cp(T.PH[0:24, :], T.P3[0:24, :], "P3", "PH")
    mm(T.b1[:, 256:400], T.PH[0:24, :], T.SX[0:24, :], True, True, "PH SX", "b1")

    iota(T.F5[:, 0:32], [[1, 4], [12, 8]], 4 + 4 * (me - min(near + [me])), 0, "F5", after="UT")
    iota(T.KB[:, :], [[1, 8], [0, 4], [8, 4]], 0, -1, "KB", after="F5")
    iota(T.FK[:, :], [[-32, 8], [-8, 5]], 5, 2, "FK", after="KB")
    iota(T.FB[:, :], [[-48, 8], [-9, 5]], -3, 3, "FB", after="FK")
    cp(T.L5[:, 0:32], T.F5[:, 0:32], "F5", "L5")
    LD = T.L5[:, 32:40]
    ts(LD, T.M2[:, 0:8], 2.5, mult, "M2", "LD", 41.5, add)
    ts(T.CX[:, 6:7], T.PO[:, 0:1], 3.0, add, "PR0 PO", "CX6", T.PR[:, 0:1], sub)
    ts(T.CX[:, 7:8], T.CX[:, 6:7], 6.0, eq, "CX6", "CX7")
    ts(T.CX[:, 0:1], T.CX[:, 6:7], 6.0, op.not_equal, "CX6", "CX0", 0.5, mult)
    sc(T.F5[:, 32:40], T.M2[:, 0:8], "M2", "F8", bias=190.0 + 8 * (me - min(near + [me])), scale=12.0)
    ts(T.LE[:, :], T.F5[:, 32:40], T.CX[:, 6:7], add, "F8 CX6 CX0", "LE", T.CX[:, 0:1], mult)
    sfill(T.R5[:, :], -BIG, "R5")
    sc(T.R5[:, 0::5], T.M2[:, 0:8], "M2", "R5", bias=15.0 / 64 - 0.5, scale=1.0 / 64)
    for ap, w in ((T.GV0[:, :], "GV0"), (T.GV1[:, :], "GV1"), (T.HV0[:, :], "HV0"), (T.GX[:, 0:1], "GX0"), (T.HX[:, 0:1], "HX0"),
                  (T.NW[:, 0:OFF], "NWp0"), (T.NW[:, TOP:W], "NWp1"), (T.GTB[:, :], "GTB"), (T.SC[:, :], "SC")):
        sfill(ap, 0.0, w)
    fill(T.GLB[:, :], 0, "GLB")
    fill(T.PW[:, 0:OFF], 0, "PWb0")
    fill(T.PW[:, TOP:W], 0, "PWb1")
    small(T.RK[:, :], T.FK[:, :], 8, "FK", "RK")
    sfill(T.RK[:, 0::5], 0.0, "RK")
    small(T.RN1[:, :], T.FB[:, :], 8, "FB", "RN1")
    ts(T.RN2[:, :], T.FB[:, :], 3.0, eq, "FB", "RN2")
    tt(T.RN0[:, :], T.RN1[:, :], T.RN2[:, :], sub, "RN1 RN2", "RN0")
    for a, b in (("RNA", "RN0"), ("RNB", "RN1")):
        tt(T[a][:, 0:39], T[b][:, 0:39], T[b][:, 1:40], sub, b, a)
        sc(T[a][:, 4::5], T[b][:, 4::5], b, a)
    ts(T.IDF[:, :], T.DC[:, :], 0.0, eq, "DC", "IDF")
    sc(T.IDH[:, :], T.IDF[:, :], "IDF", "IDH")
    sc(T.GSH[:, :], GS, "GS48", "GSH")
    sc(T.GSF[:, :], GS, "GS48", "GSF")
    sc(T.MIH[0:16, :], T.MI[0:16, :], "MI", "MIH")
    for f in range(4):
        sc(T.SC[:, 2 + 4 * f:128:16], GS, "GS48 SC", "SC%d" % f)

    def closing():
        iota(T.CI[:, 0:1], [[0, 1]], 0, 1, "CI0", True, "net")
        iota(T.IC[:, :], [[1, 128]], 0, 0, "IC", True, "net")
        for k, ops in enumerate(((15, an), (4, rs), (7, an), (1, an), (1, rs, 7, an))):
            ts(T.CI[:, k + 1:k + 2], T.CI[:, 0:1], ops[0], ops[1], "CI0", "CI%d" % (k + 1), *ops[2:])
        cp(T.CF[:, 0:6], T.CI[:, 0:6], "CI0 CI1 CI2 CI3 CI4 CI5", "CF")
        p15, pg, p7, p1, ph = [T.CF[:, k:k + 1] for k in range(1, 6)]
        ts(T.CX[:, 1:2], p15, 8.0, mult, "CF", "CX1", pg, add)
        ts(T.CX[:, 2:3], p1, 8.0, mult, "CF", "CX2", pg, add)
        ts(T.CX[:, 4:5], T.CX[:, 2:3], 2.0, mult, "CX2", "CX4", -15.0, add)
        ts(T.CX[:, 3:4], p7, 5.0, mult, "CF", "CX3", -22.0, add)
        ts(T.IDP[:, :], T.IC[:, :], T.CX[:, 1:2], eq, "IC CX1", "IDP")
        sc(T.IDQ[:, :], T.IDP[:, :], "IDP", "IDQ")
        ts(T.MIP[:, :], T.M2[:, :], T.CX[:, 4:5], eq, "M2 CX4", "MIP")
        ts(T.GSP[:, :], T.IC[:, 0:8], ph, eq, "IC CF", "GSP")
        ts(T.LP[:, :], T.C26[:, :], T.CX[:, 3:4], add, "C26 CX3", "LP")
        ts(T.IC3[:, :], T.IC[:, :], 3, rs, "IC", "IC3")
        ts(T.MI8[:, :], T.IC3[:, :], p15, eq, "IC3 CF", "MI8")

    ts(T.NA[0:80, :], T.NT[0:80, :], 10, rs, "NT0 NT1", "NA")
    ts(T.NP[0:80, 64:128], T.NT[0:80, :], 63, an, "NT0 NT1", "NP1")
    ts(T.NU[0:80, :], T.NA[0:80, :], float(me), eq, "NA", "NU", FAR - rel, mult)
    ts(T.NP[0:80, 0:64], T.NT[0:80, :], 8192 - 64, an, "NT0 NT1", "NP0")
    cp(T.NS[0:80, 64:128], T.NP[0:80, 64:128], "NP1", "NS1")
    ts(T.NS[0:80, 128:192], T.NU[0:80, :], float(-FAR), add, "NU", "NS2")
    tt(T.NS[0:80, 0:64], T.NP[0:80, 0:64], T.NS[0:80, 128:192], sub, "NP0 NS2", "NS0")
    for b in (1, 2, 0):
        dma("y", "lnd", T.ND[b:15:3, :], T.NS[0:80, 64 * b:64 * b + 64], "NS%d" % b)
    event("lnd", 3 * 16, "ND", 1.9)
    for k in range(4, 8):
        dma("y", "lpl", T.PW[16 * k:16 * k + 16, OFF:TOP], T.planes[:, :], "", "lnd")
    event("lpl", 128, "PWa", 2 * LOCAL)
    for b in range(4):
        bank = "b0" if b % 2 else "b2"
        mm(T[bank][:, 0:256], T.MIH[0:15, :], T.ND[0:15, 256 * b:256 * b + 256], True, True, "MIH ND", bank)
        (cp if b % 2 else sc)(T.NW[:, OFF + 256 * b:OFF + 256 * b + 256], T[bank][:, 0:256], bank, "NW%d" % b)

    ts(T.SB[0:32, :], T.KB[0:32, :], 0.0, eq, "KB", "SB")
    cp(T.PQH[0:24, :], T.PQ[0:24, :], "PQ", "PQH")
    for bank, src, out in (("b3", "PQH", "HTB"), ("b4", "PH", "HTA")):
        mm(T[bank][:, 0:128], T.SB[0:24, :], T[src][0:24, :], True, True, "SB " + src, bank)
        sc(T[out][:, :], T[bank][:, 0:128], bank + " CX7", out, bias=T.CX[:, 7:8], f=act.Identity)

    def opened():
        mm(T.b6[:, 0:48], T.ONF[0:1, :], T.CY[0:1, :], True, False, "ONF " + cy, "b6", True)

    def slots(a, out, rhs, r, bank):
        h = a % 2
        at = a + 128 * (1 - h)
        mm(out, T.AA[:, at:at + 249:8], rhs, not h, bool(h), "AA AA0 AA1 " + r, bank)

    def dispatch(k):
        ms, end = "MS%d" % k, k == R - 1
        small(T.OH[:, :], T.b6[:, 0:48], TT, "b6", "OH")
        mm(T.b7[:, 0:48], T.UT[:, :], T.OH[:, :], True, True, "UT OH", "b7")
        tt(T.BT[:, 0::4], T.b6[:, 0:48], T.OH[:, :], mult, "b6 OH", "BT0")
        for c in range(3):
            tt(T.BT[:, 1 + c::4], T.b1[:, 256 + 48 * c:304 + 48 * c], T.OH[:, :], mult, "b1 OH", "BT%d" % (c + 1))
        scan(T.SS[:, :], T.R6[:, :], T.b7[:, 0:48], 0.0, mult, hi, "R6 b7", "SS")
        tt(T.AA[:, 128:256], T.SS[:, :], T.IA[:, :], eq, "SS LA IA", "AA", T.LA[:, 0:8])
        for a in range(8):
            slots(a, T.b7[32 * (a // 2):32 * (a // 2) + 32, 64:88], T.BT[:, 24 * a:24 * a + 24], "BT0 BT1 BT2 BT3", "b7")
        cp(T[ms][:, :], T.b7[:, 64:88], "b7", ms)
        block = lambda i: 4 * min((far, near + [me])[i])
        spread(lambda i: T[ms][:, block(i):block(i) + 12], lambda q: T["LH%d" % k][:, 12 * slot(q, me):12 * slot(q, me) + 12], "rq%d" % k,
               ms + " RL%d0" % k, "LH%d" % k, 0.0 if k else FIRST)
        cp(T["LM%d" % k][:, 4:64], T["LH%d" % k][:, :], "LH%d" % k, "LM%d" % k)
        ts(T.HL[:, :], T.b6[:, me:48:6], MID + OFF, add, "b6", "HL", float(TOP), lo)
        sc(T.QI[:, :], T.b6[:, 0:48:6], "b6 BT0 HL", "QI", bias=QB, scale=1.0 / TT)
        tt(T.DQ[:, :], T.QI[:, :], T["MIP" if end else "MI"][:, :], mult, "QI LT MI MIP" if end else "QI LT MI", "DQ", T.LT[:, 0:8])
        mm(T.b5[:, 0:8], T.DQ[:, :], T["GSP" if end else "GSH"][:, :], True, True, "DQ GSH GSP" if end else "DQ GSH", "b5")
        ts(T.LI[:, :], T.b5[:, 0:8], 5.0, mult, "b5", "LI", 2 - 5 * QB, add)
        ident = "IDQ" if end else "IDH"
        for a in range(8):
            slots(a, T.b5[32 * (a // 2):32 * (a // 2) + 32, 0:128], T[ident][:, :], ident, "b5")
        sc(T.AT[:, :], T.b5[:, 0:128], "b5", "AT")

    def step(h, i, lst, ln, pt, n, m, kept=False, turned=False, z=None):
        bk, bn = ("b3", "b4") if h == "H" else ("b0", "b1")
        X = lambda a: T[h + a]
        e = 5 * m
        if kept:
            mm(T[bn][0:n, 0:e], T.IDF[0:n, 0:n], X("V0")[0:n, 0:e], True, False, "IDF " + h + "V0", bn, True)
        sc(X("N")[:, 0:n], T.NW[:, :], "NWp0 NWp1 NW0 NW1 NW2 NW3 " + ln, h + "N", by=lst)
        tt(X("P")[:, 0:n], T.PW[:, :], T[pt][:, 0:n], mult, "PWa PWb0 PWb1 " + ln + " " + pt, h + "P", lst)
        mm(T[bk][0:n, 0:e], X("P")[0:16 * m, 0:n], T.RK[0:16 * m, 0:e], True, True, h + "P RK", bk, True)
        rn = "RNB" if i == S - 1 else "RNA"
        mm(T[bn][0:n, 0:e], X("N")[0:16 * m, 0:n], T[rn][0:16 * m, 0:e], not kept, not turned, h + "N " + rn, bn)
        if turned:
            mm(T[bn][0:n, 0:25:5], T.GDF[0:80, :], T.GS48[0:80, 0:30:6], False, True, "GDF GS48", bn, True)
        scan(X("S")[0:n, 0:e], T.R5[0:n, 0:e], T[bk][0:n, 0:e], -1.0, hi, lo, "R5 " + bk, h + "S")
        tt(X("X")[0:n, 1:e], X("S")[0:n, 1:e], X("S")[0:n, 0:e - 1], eq, h + "S", h + "X")
        z = z or h + "Z"
        scan(T[z][0:n, 0:e], X("X")[0:n, 0:e], T[bn][0:n, 0:e], 0.0, mult, add, h + "X " + h + "X0 " + bn, z)
        return T[z][0:n, 4:e:5]

    def left(out, z, r, w):
        sc(out, z, r, w, bias=float(-FAR), f=act.Relu)

    def home(k):
        hl = T.HL[:, 0:8]
        z = step("H", 0, hl, "HL", "HTB", 128, 8)
        ts(hl, z, float(TOP), lo, "HZ", "HL")
        left(T.HV0[:, 0::5], z, "HZ", "HV0")
        z = step("H", 1, hl, "HL", "HTA", 128, 8)
        ts(hl, z, float(TOP), lo, "HZ", "HL")
        if k < R - 1:
            for q in range(N):
                left(T.HV1[:, q::6], z, "HZ", "HV1%d" % q)
            opened()
            mm(T.b6[:, 0:48], T.IDF[:, :], T.HV1[:, :], False, False, "IDF " + " ".join("HV1%d" % q for q in range(N)), "b6", True)
        else:
            left(T.HV1[:, 0::6], z, "HZ", "HV10")
            mm(T.b6[0:8, 0:128], T.HV1[:, 0::6], T.IDP[:, :], True, False, "IDP HV10", "b6", True)
        step("H", 2, hl, "HL", "HTB", 128, 8, kept=True)
        if k < R - 1:
            tt(T.DX[:, :], T.HZ[:, :], T.MI[:, :], mult, "HZ LD MI", "DX", LD)
            mm(T.b6[:, 0:48], T.DX[:, :], T.GS48[:, :], False, False, "DX GS48", "b6", True)
        else:
            tt(T.DX[:, :], T.HZ[:, :], T.MI8[:, :], mult, "HZ LP MI8", "DX", T.LP[:, 0:8])
            mm(T.b6[0:8, 0:128], GS, T.DX[:, :], False, False, "DX GS48", "b6", True)

    def guests(k):
        lm, rt = "LM%d" % k, "RT%d" % k
        win, ga, gb = T[lm][:, :], T.GLA[:, 0:5], T.GLB[:, 0:8]
        sc(T.GE[:, :], win, lm + " %s0 LE" % lm, "GE", by=T.LE[:, 0:5])
        tt(T.GD[:, :], win, T.MI[:, 0:80], mult, lm + " %s0 L5 MI" % lm, "GD", T.L5[:, 0:5])
        mm(T.b2[0:80, 0:8], T.GD[:, :], T.GSF[:, :], True, True, "GD GSF", "b2")
        for a, bank, copy in ((0, "b7", sc), (64, "b0", cp)):
            mm(T[bank][0:80, 0:64], T.GE[:, :], T.IDH[:, a:a + 64], True, True, "GE IDH", bank)
            copy(T.GTB[0:80, a:a + 64], T[bank][0:80, 0:64], bank + " GTB", "GTB%d" % a)
        ts(T.GLB[0:80, :], T.b2[0:80, 0:8], MID + OFF, add, "b2", "GLB")
        for c in range(3):
            tt(T.GY[:, 80 * c:80 * c + 80], win, T.MI[:, 0:80], mult, lm + " %s0 L5 MI" % lm, "GY%d" % c, T.L5[:, 8 * c + 8:8 * c + 13])
            mm(T.b2[:, 0:80], T.SC[:, 2 - c:130 - c], T.GY[:, 80 * c:80 * c + 80], c == 0, c == 2, "SC SC0 SC1 SC2 SC3 GY%d" % c, "b2")
        sc(T.GTA[:, :], T.b2[:, 0:80], "b2 CX7", "GTA", bias=T.CX[:, 7:8], f=act.Identity)
        z = step("G", 0, gb, "GLB GTB0 GTB64", "GTB", 128, 5)
        ts(ga, z, float(TOP), lo, "GZ", "GLA")
        left(T.GV0[:, 0:25:5], z, "GZ", "GV0")
        z = step("G", 1, ga, "GLA", "GTA", 80, 8)
        ts(T.GLB[0:80, :], z, float(TOP), lo, "GZ", "GLB")
        left(T.GV1[0:80, :], z, "GZ", "GV1")
        tt(T.GDF[:, :], T.GV1[:, :], T.MI[:, :], mult, "GV1 LT MI", "GDF", T.LT[:, 0:8])
        step("G", 2, gb, "GLB GTB0 GTB64", "GTB", 128, 5, kept=True, turned=True, z=rt)
        cp(T["RC%d" % k][:, 0:5], T[rt][:, 4::5], rt, "RC%d" % k)
        at = lambda q: 5 * me + 2 - slot(me, q) % 3
        spread(lambda i: T["RC%d" % k][:, 3 * i:3 * i + 3], lambda q: T["RL%d" % k][:, at(q):at(q) + 3], "rt%d" % k, "RC%d RC%d0" % (k, k), "RL%d" % k)

    def replies(k):
        tt(T.XR[:, :], T["RL%d" % k][:, :], T.AT[:, :], mult, "RL%d RL%d0 LI AT" % (k, k), "XR", T.LI[:, 0:8])
        if k < R - 1:
            mm(T.b6[:, 0:48], T.XR[:, :], T.GS48[:, :], False, True, "XR GS48", "b6", True)
        else:
            mm(T.b6[0:8, 0:128], GS, T.XR[:, :], False, True, "XR GS48", "b6", True)

    opened()
    tt(T.DX[:, :], T.T0I[:, :], T.MI[:, :], mult, "T0I LT MI", "DX", T.LT[:, 0:8])
    mm(T.b6[:, 0:48], T.DX[:, :], T.GS48[:, :], False, True, "DX GS48", "b6", True)
    for k in range(R):
        dispatch(k)
        guests(k)
        if k == 0:
            closing()
        home(k)
        replies(k)
    cp(T.YS[0:8, :], T.b6[0:8, 0:128], "b6", "YS")
    dma("y", "sty", T.y[:, :], T.YS[0:8, :], "YS")

    for i in in_order(calls):
        issue[i]()

    g.wait_ge(T.sem.sty, 16)
    g.wait_ge(T.sem.sent, sent[0])
    for q in "vtsc":
        if known["c"].get(q, 0) < count[q]:
            g.wait_ge(T.sem[q], count[q])
